import numpy as np
import ml_dtypes


def mxq(x, axis, fmt="e4m3"):
    dtype, down = {"e4m3": (ml_dtypes.float8_e4m3fn, 7), "e5m2": (ml_dtypes.float8_e5m2, 14)}[fmt]
    v = np.moveaxis(np.asarray(x, np.float32).astype(ml_dtypes.bfloat16).astype(np.float64), axis, -1)
    blocks = v.reshape(v.shape[:-1] + (-1, 32))
    amax = np.abs(blocks).max(-1, keepdims=True)
    byte = np.maximum(np.where(amax > 0, np.frexp(amax)[1] - 1 + 127, 0) - down, 1)
    scale = np.exp2(byte - 127.0)
    codes = (blocks / scale).astype(np.float32).astype(dtype).astype(np.float64)
    return np.moveaxis((codes * scale).reshape(v.shape), -1, axis)


WIDE = False


def mx_kscale(k):
    if not WIDE:
        return np.ones(k)
    levels = np.array([10, -10, 5, -5, 0])
    if k % 512:
        return np.exp2(np.random.permutation(np.resize(levels, k // 32))).repeat(32)
    a = np.empty((k // 512, 16))
    for p in range(k // 512):
        a[p, :8] = np.random.permutation(np.resize(levels, 8))
        for g in range(8):
            far = levels[np.abs(levels - a[p, g]) >= 10]
            a[p, g + 8] = far[np.random.randint(len(far))]
    return np.exp2(a.ravel()).repeat(32)


def f64(x):
    return np.asarray(x).astype(np.float64)


def striped8(idx):
    return np.concatenate([x.reshape(-1, 16).T for x in idx]).astype(np.uint16)


def runs(offs, k):
    lists = np.stack([offs[16 * r : 16 * r + 16].T.reshape(-1) for r in range(8)]).astype(np.int64)
    return lists[np.arange(k) % 512 // 64]


def pack_weight(w):
    k, n = w.shape
    w = f64(np.asarray(w, np.float32).astype(ml_dtypes.bfloat16)).reshape(k // 32, 32, n)
    amax = np.abs(w).max(1)
    byte = np.clip(np.where(amax > 0, np.frexp(amax)[1] - 1 + 127 - 7, 1), 1, 254)
    scaled = (w * np.exp2(127.0 - byte)[:, None, :]).reshape(k, n).astype(np.float32)
    words = np.ascontiguousarray(scaled.reshape(k // 512, 128, 4, n).transpose(0, 1, 3, 2)).astype(ml_dtypes.float8_e4m3fn).view(np.uint8)
    return words, np.ascontiguousarray(byte.astype(np.uint8).reshape(k // 512, 16, n))


def unpack_weight(words, scales):
    g, p, n, _ = words.shape
    vals = np.ascontiguousarray(words).view(ml_dtypes.float8_e4m3fn).astype(np.float64) * np.repeat(np.exp2(scales.astype(np.float64) - 127.0), 8, axis=1)[..., None]
    return vals.transpose(0, 1, 3, 2).reshape(g * 512, n)


E2M1 = np.array([0.0, 0.5, 1.0, 1.5, 2.0, 3.0, 4.0, 6.0, -0.0, -0.5, -1.0, -1.5, -2.0, -3.0, -4.0, -6.0])


def pack_fp4(w):
    k, n = w.shape
    w = f64(np.asarray(w, np.float32).astype(ml_dtypes.bfloat16)).reshape(k // 32, 32, n)
    amax = np.abs(w).max(1)
    mant, ex = np.frexp(amax / 6.0)
    byte = np.clip(np.where(amax > 0, np.where(mant > 0.5, ex, ex - 1) + 127, 1), 1, 254)
    scaled = (w * np.exp2(127.0 - byte)[:, None, :]).reshape(k, n).astype(np.float32)
    c = np.ascontiguousarray(scaled.reshape(k // 512, 128, 4, n).transpose(0, 1, 3, 2)).astype(ml_dtypes.float4_e2m1fn).view(np.uint8) & 0xF
    words = (c[..., 0::2] | (c[..., 1::2] << 4)).reshape(k // 512, 128, 2 * n)
    return np.ascontiguousarray(words), np.ascontiguousarray(byte.astype(np.uint8).reshape(k // 512, 16, n))


def unpack_fp4(words, scales):
    g, _, n = scales.shape
    words = np.ascontiguousarray(words).reshape(g, 128, n, 2)
    nib = np.empty((g, 128, n, 4), np.uint8)
    nib[..., 0::2] = words & 0xF
    nib[..., 1::2] = words >> 4
    vals = E2M1[nib] * np.repeat(np.exp2(scales.astype(np.float64) - 127.0), 8, axis=1)[..., None]
    return vals.transpose(0, 1, 3, 2).reshape(g * 512, n)


def gelu(v):
    return 0.5 * v * (1.0 + np.tanh(np.sqrt(2.0 / np.pi) * (v + 0.044715 * v**3)))


K, T, S, H, N = 512, 2048, 512, 512, 128


def setup_inputs():
    n = np.random.standard_normal
    s = mx_kscale(K)[:, None]
    u = mx_kscale(H)
    packed_xT = pack_weight(n((K, T)) * s)
    packed_w1 = pack_fp4(n((K, N)) / np.sqrt(2 * K) / s)
    packed_w3 = pack_fp4(n((H, N)) / np.sqrt(2 * H) / u[:, None])
    return {
        "x_words": packed_xT[0],
        "x_scales": packed_xT[1],
        "w1_words": packed_w1[0],
        "w1_scales": packed_w1[1],
        "w2": (n((K, H)) / np.sqrt(K) / s * u).astype(np.float32),
        "w3_words": packed_w3[0],
        "w3_scales": packed_w3[1],
        "offs": striped8(np.stack([np.random.permutation(T)[:S] for _ in range(8)])),
    }


def reference(x_words, x_scales, w1_words, w1_scales, w2, w3_words, w3_scales, offs):
    xq = unpack_weight(x_words, x_scales)[np.arange(K)[:, None], runs(offs, K)]
    h = gelu(mxq(f64(w2), 0, "e4m3").T @ xq)
    return unpack_fp4(w1_words, w1_scales).T @ xq + unpack_fp4(w3_words, w3_scales).T @ mxq(h, 0, "e4m3")

@@ -1,0 +1,108 @@
+from contextlib import ExitStack
+
+import concourse.mybir as mybir
+
+F32 = mybir.dt.float32
+BF16 = mybir.dt.bfloat16
+I32 = mybir.dt.int32
+U32 = mybir.dt.uint32
+U16 = mybir.dt.uint16
+U8 = mybir.dt.uint8
+FP8X4 = mybir.dt.float8_e4m3fn_x4
+FP4X4 = mybir.dt.float4_e2m1fn_x4
+GELU = mybir.ActivationFunctionType.Gelu_apprx_tanh
+
+P = 128
+K, T, S, H, N = 512, 2048, 512, 512, 128
+PACK = 4
+CHUNK = 128
+HALF = 256
+M_VECTOR = 80
+FLOPS = 2 * S * (K * H + K * N + H * N)
+
+
+def tile_picked_phlora_gelu_p_kernel(tc, x_words, x_scales, w1_words, w1_scales, w2, w3_words, w3_scales, offs, out):
+    nc = tc.nc
+    with ExitStack() as ctx:
+        keep = ctx.enter_context(tc.tile_pool(name="keep", bufs=1))
+        psum = ctx.enter_context(tc.psum_pool(name="psum", bufs=1))
+
+        offsets = keep.tile([P, S // 16], U16, name="offsets")
+        nc.sync.dma_start(offsets[:], offs)
+
+        w2_raw = keep.tile([P, PACK, H], F32, name="w2_raw", align_bytes=64)
+        nc.sync.dma_start(w2_raw[:], w2.rearrange("(p j) c -> p j c", j=PACK))
+
+        word_table = keep.tile([P, T], I32, name="word_table", align_bytes=64)
+        nc.sync.dma_start(word_table[:], x_words[0].rearrange("p n t -> p (n t)").bitcast(I32))
+
+        scale_table = keep.tile([P, T], U8, name="scale_table", tag="scale_slot", align_bytes=64)
+        nc.vector.memset(scale_table[:].bitcast(I32), 0)
+        nc.scalar.dma_start(scale_table[0:P:8, :].bitcast(I32), x_scales[0].bitcast(I32))
+
+        w1_codes = keep.tile([P, 2 * N], U8, name="w1_codes", align_bytes=64)
+        nc.sync.dma_start(w1_codes[:].bitcast(I32), w1_words[0].bitcast(I32))
+        w3_codes = keep.tile([P, 2 * N], U8, name="w3_codes", align_bytes=64)
+        nc.sync.dma_start(w3_codes[:].bitcast(I32), w3_words[0].bitcast(I32))
+
+        w1_plane = keep.tile([P, N], U8, name="w1_plane", align_bytes=64)
+        nc.gpsimd.memset(w1_plane[:].bitcast(I32), 0)
+        for i in range(4):
+            nc.gpsimd.dma_start(w1_plane[i:P:32, :].bitcast(I32), w1_scales[0, i:16:4, :].bitcast(I32))
+
+        x_plane = keep.tile([P, S], U8, name="x_plane", align_bytes=64)
+        nc.vector.memset(x_plane[:].bitcast(I32), 0)
+        picked_scales = keep.tile([P, S], U8, name="picked_scales", align_bytes=64)
+        nc.vector.tensor_copy(picked_scales[:], scale_table[:].indirect(offsets[:]))
+        for i in range(4):
+            nc.scalar.dma_start(x_plane[i:P:32, :].bitcast(I32), picked_scales[8 * i:P:32, :].bitcast(I32))
+
+        w3_plane = keep.tile([P, N], U8, name="w3_plane", tag="scale_slot", align_bytes=64)
+        nc.vector.memset(w3_plane[:].bitcast(I32), 0)
+        for i in range(4):
+            nc.sync.dma_start(w3_plane[i:P:32, :].bitcast(I32), w3_scales[0, i:16:4, :].bitcast(I32))
+
+        w2_bf = keep.tile([P, PACK * H], BF16, name="w2_bf", align_bytes=64)
+        src = w2_raw[:].rearrange("p j (m t) -> p m t j", t=PACK)
+        dst = w2_bf[:].rearrange("p (t m j) -> p m t j", t=PACK, j=PACK)
+        nc.vector.tensor_copy(dst[:, :M_VECTOR], src[:, :M_VECTOR])
+        nc.scalar.copy(dst[:, M_VECTOR:], src[:, M_VECTOR:])
+        w2_codes = keep.tile([P, H], U32, name="w2_codes", align_bytes=64)
+        w2_plane = keep.tile([P, H], U8, name="w2_plane", align_bytes=64)
+        nc.vector.quantize_mx(out=w2_codes[:].bitcast(FP8X4), scales=w2_plane[:], in_=w2_bf[:])
+
+        picked_words = []
+        for u in range(S // HALF):
+            words = keep.tile([P, HALF], U32, name=f"picked_words{u}", align_bytes=64)
+            nc.vector.tensor_copy(words[:], word_table[:].bitcast(U32).indirect(offsets[:, u * HALF // 16:(u + 1) * HALF // 16]))
+            picked_words.append(words)
+
+        def x_operand(c):
+            u, lo = divmod(c * CHUNK, HALF)
+            return picked_words[u][:, lo:lo + CHUNK].bitcast(FP8X4), x_plane[:, c * CHUNK:(c + 1) * CHUNK]
+
+        hidden = []
+        for c in range(S // CHUNK):
+            x_codes, x_bytes = x_operand(c)
+            pre = psum.tile([P, PACK, CHUNK], F32, name=f"pre{c}")
+            for t in range(PACK):
+                cols = slice(t * P, (t + 1) * P)
+                nc.tensor.matmul_mx(out=pre[:, t, :], lhsT=w2_codes[:, cols].bitcast(FP8X4), lhsT_scale=w2_plane[:, cols],
+                                    rhs=x_codes, rhs_scale=x_bytes, start=True, stop=True)
+            h = keep.tile([P, CHUNK * PACK], BF16, name=f"h{c}", align_bytes=64)
+            nc.scalar.activation(h[:].rearrange("p (n t) -> p n t", t=PACK), pre[:].rearrange("p t n -> p n t"), GELU)
+            hidden.append(h)
+
+        for c in range(S // CHUNK):
+            x_codes, x_bytes = x_operand(c)
+            h_codes = keep.tile([P, CHUNK], U32, name=f"h_codes{c}", align_bytes=64)
+            h_plane = keep.tile([P, CHUNK], U8, name=f"h_plane{c}", align_bytes=64)
+            nc.vector.quantize_mx(out=h_codes[:].bitcast(FP8X4), scales=h_plane[:], in_=hidden[c][:])
+            acc = psum.tile([P, CHUNK], F32, name=f"acc{c}")
+            nc.tensor.matmul_mx(out=acc[:], lhsT=w1_codes[:].bitcast(FP4X4), lhsT_scale=w1_plane[:],
+                                rhs=x_codes, rhs_scale=x_bytes, start=True, stop=False)
+            nc.tensor.matmul_mx(out=acc[:], lhsT=w3_codes[:].bitcast(FP4X4), lhsT_scale=w3_plane[:],
+                                rhs=h_codes[:].bitcast(FP8X4), rhs_scale=h_plane[:], start=False, stop=True)
+            result = keep.tile([P, CHUNK], F32, name=f"result{c}", align_bytes=64)
+            nc.vector.tensor_copy(result[:], acc[:])
+            nc.sync.dma_start(out[:, c * CHUNK:(c + 1) * CHUNK], result[:])

@@ -17,7 +17,7 @@ K, T, S, H, N = 512, 2048, 512, 512, 128
 PACK = 4
 CHUNK = 128
 HALF = 256
-M_VECTOR = 80
+M_VECTOR = 92
 FLOPS = 2 * S * (K * H + K * N + H * N)
 
 
@@ -27,40 +27,42 @@ def tile_picked_phlora_gelu_p_kernel(tc, x_words, x_scales, w1_words, w1_scales,
         keep = ctx.enter_context(tc.tile_pool(name="keep", bufs=1))
         psum = ctx.enter_context(tc.psum_pool(name="psum", bufs=1))
 
-        offsets = keep.tile([P, S // 16], U16, name="offsets")
-        nc.sync.dma_start(offsets[:], offs)
+        scale_table = keep.tile([P, T], U8, name="scale_table", tag="scale_slot", align_bytes=64)
+        nc.vector.memset(scale_table[:].bitcast(I32), 0)
+        warm_in = keep.tile([P, 1], F32, name="warm_in")
+        nc.vector.memset(warm_in[:], 0.0)
+        warm_out = keep.tile([P, 1], F32, name="warm_out")
+        nc.scalar.activation(warm_out[:], warm_in[:], GELU)
+        x_plane = keep.tile([P, S], U8, name="x_plane", align_bytes=64)
+        nc.vector.memset(x_plane[:].bitcast(I32), 0)
 
         w2_raw = keep.tile([P, PACK, H], F32, name="w2_raw", align_bytes=64)
-        nc.sync.dma_start(w2_raw[:], w2.rearrange("(p j) c -> p j c", j=PACK))
+        w2_rows = w2.rearrange("(p j) c -> p j c", j=PACK)
+        nc.sync.dma_start(w2_raw[:, :1], w2_rows[:, :1])
+        offsets = keep.tile([P, S // 16], U16, name="offsets")
+        nc.sync.dma_start(offsets[:], offs)
+        nc.sync.dma_start(scale_table[0:P:8, :].bitcast(I32), x_scales[0].bitcast(I32))
+        nc.sync.dma_start(w2_raw[:, 1:], w2_rows[:, 1:])
 
         word_table = keep.tile([P, T], I32, name="word_table", align_bytes=64)
         nc.sync.dma_start(word_table[:], x_words[0].rearrange("p n t -> p (n t)").bitcast(I32))
-
-        scale_table = keep.tile([P, T], U8, name="scale_table", tag="scale_slot", align_bytes=64)
-        nc.vector.memset(scale_table[:].bitcast(I32), 0)
-        nc.scalar.dma_start(scale_table[0:P:8, :].bitcast(I32), x_scales[0].bitcast(I32))
 
         w1_codes = keep.tile([P, 2 * N], U8, name="w1_codes", align_bytes=64)
         nc.sync.dma_start(w1_codes[:].bitcast(I32), w1_words[0].bitcast(I32))
         w3_codes = keep.tile([P, 2 * N], U8, name="w3_codes", align_bytes=64)
         nc.sync.dma_start(w3_codes[:].bitcast(I32), w3_words[0].bitcast(I32))
 
-        w1_plane = keep.tile([P, N], U8, name="w1_plane", align_bytes=64)
-        nc.gpsimd.memset(w1_plane[:].bitcast(I32), 0)
-        for i in range(4):
-            nc.gpsimd.dma_start(w1_plane[i:P:32, :].bitcast(I32), w1_scales[0, i:16:4, :].bitcast(I32))
-
-        x_plane = keep.tile([P, S], U8, name="x_plane", align_bytes=64)
-        nc.vector.memset(x_plane[:].bitcast(I32), 0)
         picked_scales = keep.tile([P, S], U8, name="picked_scales", align_bytes=64)
         nc.vector.tensor_copy(picked_scales[:], scale_table[:].indirect(offsets[:]))
         for i in range(4):
-            nc.scalar.dma_start(x_plane[i:P:32, :].bitcast(I32), picked_scales[8 * i:P:32, :].bitcast(I32))
+            (nc.sync, nc.scalar)[i % 2].dma_start(x_plane[i:P:32, :].bitcast(I32), picked_scales[8 * i:P:32, :].bitcast(I32))
 
-        w3_plane = keep.tile([P, N], U8, name="w3_plane", tag="scale_slot", align_bytes=64)
-        nc.vector.memset(w3_plane[:].bitcast(I32), 0)
-        for i in range(4):
-            nc.sync.dma_start(w3_plane[i:P:32, :].bitcast(I32), w3_scales[0, i:16:4, :].bitcast(I32))
+        fp4_planes = keep.tile([P, 2 * N], U8, name="fp4_planes", tag="scale_slot", align_bytes=64)
+        nc.vector.memset(fp4_planes[:].bitcast(I32), 0)
+        w1_plane, w3_plane = fp4_planes[:, :N], fp4_planes[:, N:]
+        for plane, rows in ((w1_plane, w1_scales), (w3_plane, w3_scales)):
+            for i in range(4):
+                nc.sync.dma_start(plane[i:P:32, :].bitcast(I32), rows[0, i:16:4, :].bitcast(I32))
 
         w2_bf = keep.tile([P, PACK * H], BF16, name="w2_bf", align_bytes=64)
         src = w2_raw[:].rearrange("p j (m t) -> p m t j", t=PACK)
@@ -99,9 +101,9 @@ def tile_picked_phlora_gelu_p_kernel(tc, x_words, x_scales, w1_words, w1_scales,
             h_plane = keep.tile([P, CHUNK], U8, name=f"h_plane{c}", align_bytes=64)
             nc.vector.quantize_mx(out=h_codes[:].bitcast(FP8X4), scales=h_plane[:], in_=hidden[c][:])
             acc = psum.tile([P, CHUNK], F32, name=f"acc{c}")
-            nc.tensor.matmul_mx(out=acc[:], lhsT=w1_codes[:].bitcast(FP4X4), lhsT_scale=w1_plane[:],
+            nc.tensor.matmul_mx(out=acc[:], lhsT=w1_codes[:].bitcast(FP4X4), lhsT_scale=w1_plane,
                                 rhs=x_codes, rhs_scale=x_bytes, start=True, stop=False)
-            nc.tensor.matmul_mx(out=acc[:], lhsT=w3_codes[:].bitcast(FP4X4), lhsT_scale=w3_plane[:],
+            nc.tensor.matmul_mx(out=acc[:], lhsT=w3_codes[:].bitcast(FP4X4), lhsT_scale=w3_plane,
                                 rhs=h_codes[:].bitcast(FP8X4), rhs_scale=h_plane[:], start=False, stop=True)
             result = keep.tile([P, CHUNK], F32, name=f"result{c}", align_bytes=64)
             nc.vector.tensor_copy(result[:], acc[:])

@@ -17,7 +17,7 @@ K, T, S, H, N = 512, 2048, 512, 512, 128
 PACK = 4
 CHUNK = 128
 HALF = 256
-M_VECTOR = 92
+M_VECTOR = 88
 FLOPS = 2 * S * (K * H + K * N + H * N)
 
 
@@ -47,19 +47,17 @@ def tile_picked_phlora_gelu_p_kernel(tc, x_words, x_scales, w1_words, w1_scales,
         word_table = keep.tile([P, T], I32, name="word_table", align_bytes=64)
         nc.sync.dma_start(word_table[:], x_words[0].rearrange("p n t -> p (n t)").bitcast(I32))
 
-        w1_codes = keep.tile([P, 2 * N], U8, name="w1_codes", align_bytes=64)
-        nc.sync.dma_start(w1_codes[:].bitcast(I32), w1_words[0].bitcast(I32))
-        w3_codes = keep.tile([P, 2 * N], U8, name="w3_codes", align_bytes=64)
-        nc.sync.dma_start(w3_codes[:].bitcast(I32), w3_words[0].bitcast(I32))
-
         picked_scales = keep.tile([P, S], U8, name="picked_scales", align_bytes=64)
         nc.vector.tensor_copy(picked_scales[:], scale_table[:].indirect(offsets[:]))
         for i in range(4):
-            (nc.sync, nc.scalar)[i % 2].dma_start(x_plane[i:P:32, :].bitcast(I32), picked_scales[8 * i:P:32, :].bitcast(I32))
+            nc.sync.dma_start(x_plane[i:P:32, :].bitcast(I32), picked_scales[8 * i:P:32, :].bitcast(I32))
 
-        fp4_planes = keep.tile([P, 2 * N], U8, name="fp4_planes", tag="scale_slot", align_bytes=64)
-        nc.vector.memset(fp4_planes[:].bitcast(I32), 0)
-        w1_plane, w3_plane = fp4_planes[:, :N], fp4_planes[:, N:]
+        fp4 = keep.tile([P, 6 * N], U8, name="fp4", tag="scale_slot", align_bytes=64)
+        nc.vector.memset(fp4[:, :2 * N].bitcast(I32), 0)
+        w1_plane, w3_plane = fp4[:, :N], fp4[:, N:2 * N]
+        w1_codes, w3_codes = fp4[:, 2 * N:4 * N], fp4[:, 4 * N:]
+        nc.sync.dma_start(w1_codes.bitcast(I32), w1_words[0].bitcast(I32))
+        nc.sync.dma_start(w3_codes.bitcast(I32), w3_words[0].bitcast(I32))
         for plane, rows in ((w1_plane, w1_scales), (w3_plane, w3_scales)):
             for i in range(4):
                 nc.sync.dma_start(plane[i:P:32, :].bitcast(I32), rows[0, i:16:4, :].bitcast(I32))
@@ -83,6 +81,11 @@ def tile_picked_phlora_gelu_p_kernel(tc, x_words, x_scales, w1_words, w1_scales,
             u, lo = divmod(c * CHUNK, HALF)
             return picked_words[u][:, lo:lo + CHUNK].bitcast(FP8X4), x_plane[:, c * CHUNK:(c + 1) * CHUNK]
 
+        def parts(c):
+            if c == S // CHUNK - 1:
+                return [slice(0, CHUNK // 2), slice(CHUNK // 2, CHUNK)]
+            return [slice(0, CHUNK)]
+
         hidden = []
         for c in range(S // CHUNK):
             x_codes, x_bytes = x_operand(c)
@@ -92,18 +95,20 @@ def tile_picked_phlora_gelu_p_kernel(tc, x_words, x_scales, w1_words, w1_scales,
                 nc.tensor.matmul_mx(out=pre[:, t, :], lhsT=w2_codes[:, cols].bitcast(FP8X4), lhsT_scale=w2_plane[:, cols],
                                     rhs=x_codes, rhs_scale=x_bytes, start=True, stop=True)
             h = keep.tile([P, CHUNK * PACK], BF16, name=f"h{c}", align_bytes=64)
-            nc.scalar.activation(h[:].rearrange("p (n t) -> p n t", t=PACK), pre[:].rearrange("p t n -> p n t"), GELU)
+            for part in parts(c):
+                nc.scalar.activation(h[:].rearrange("p (n t) -> p n t", t=PACK)[:, part], pre[:].rearrange("p t n -> p n t")[:, part], GELU)
             hidden.append(h)
 
         for c in range(S // CHUNK):
             x_codes, x_bytes = x_operand(c)
             h_codes = keep.tile([P, CHUNK], U32, name=f"h_codes{c}", align_bytes=64)
             h_plane = keep.tile([P, CHUNK], U8, name=f"h_plane{c}", align_bytes=64)
-            nc.vector.quantize_mx(out=h_codes[:].bitcast(FP8X4), scales=h_plane[:], in_=hidden[c][:])
+            for part in parts(c):
+                nc.vector.quantize_mx(out=h_codes[:, part].bitcast(FP8X4), scales=h_plane[:, part], in_=hidden[c][:, PACK * part.start:PACK * part.stop])
             acc = psum.tile([P, CHUNK], F32, name=f"acc{c}")
-            nc.tensor.matmul_mx(out=acc[:], lhsT=w1_codes[:].bitcast(FP4X4), lhsT_scale=w1_plane,
+            nc.tensor.matmul_mx(out=acc[:], lhsT=w1_codes.bitcast(FP4X4), lhsT_scale=w1_plane,
                                 rhs=x_codes, rhs_scale=x_bytes, start=True, stop=False)
-            nc.tensor.matmul_mx(out=acc[:], lhsT=w3_codes[:].bitcast(FP4X4), lhsT_scale=w3_plane,
+            nc.tensor.matmul_mx(out=acc[:], lhsT=w3_codes.bitcast(FP4X4), lhsT_scale=w3_plane,
                                 rhs=h_codes[:].bitcast(FP8X4), rhs_scale=h_plane[:], start=False, stop=True)
             result = keep.tile([P, CHUNK], F32, name=f"result{c}", align_bytes=64)
             nc.vector.tensor_copy(result[:], acc[:])

@@ -111,5 +111,8 @@ def tile_picked_phlora_gelu_p_kernel(tc, x_words, x_scales, w1_words, w1_scales,
             nc.tensor.matmul_mx(out=acc[:], lhsT=w3_codes.bitcast(FP4X4), lhsT_scale=w3_plane,
                                 rhs=h_codes[:].bitcast(FP8X4), rhs_scale=h_plane[:], start=False, stop=True)
             result = keep.tile([P, CHUNK], F32, name=f"result{c}", align_bytes=64)
-            nc.vector.tensor_copy(result[:], acc[:])
+            if c < 2:
+                nc.scalar.copy(result[:], acc[:])
+            else:
+                nc.vector.tensor_copy(result[:], acc[:])
             nc.sync.dma_start(out[:, c * CHUNK:(c + 1) * CHUNK], result[:])

@@ -18,6 +18,7 @@ PACK = 4
 CHUNK = 128
 HALF = 256
 M_VECTOR = 88
+WARM_M = 64
 FLOPS = 2 * S * (K * H + K * N + H * N)
 
 
@@ -27,7 +28,7 @@ def tile_picked_phlora_gelu_p_kernel(tc, x_words, x_scales, w1_words, w1_scales,
         keep = ctx.enter_context(tc.tile_pool(name="keep", bufs=1))
         psum = ctx.enter_context(tc.psum_pool(name="psum", bufs=1))
 
-        scale_table = keep.tile([P, T], U8, name="scale_table", tag="scale_slot", align_bytes=64)
+        scale_table = keep.tile([P, T], U8, name="scale_table", align_bytes=64)
         nc.vector.memset(scale_table[:].bitcast(I32), 0)
         warm_in = keep.tile([P, 1], F32, name="warm_in")
         nc.vector.memset(warm_in[:], 0.0)
@@ -35,8 +36,10 @@ def tile_picked_phlora_gelu_p_kernel(tc, x_words, x_scales, w1_words, w1_scales,
         nc.scalar.activation(warm_out[:], warm_in[:], GELU)
         x_plane = keep.tile([P, S], U8, name="x_plane", align_bytes=64)
         nc.vector.memset(x_plane[:].bitcast(I32), 0)
+        h_codes_all = keep.tile([P, S], U32, name="h_codes_all", align_bytes=64)
+        nc.vector.memset(h_codes_all[:].bitcast(I32), 0)
 
-        w2_raw = keep.tile([P, PACK, H], F32, name="w2_raw", align_bytes=64)
+        w2_raw = keep.tile([P, PACK, H], F32, name="w2_raw", tag="raw_slot", align_bytes=64)
         w2_rows = w2.rearrange("(p j) c -> p j c", j=PACK)
         nc.sync.dma_start(w2_raw[:, :1], w2_rows[:, :1])
         offsets = keep.tile([P, S // 16], U16, name="offsets")
@@ -52,21 +55,26 @@ def tile_picked_phlora_gelu_p_kernel(tc, x_words, x_scales, w1_words, w1_scales,
         for i in range(4):
             nc.sync.dma_start(x_plane[i:P:32, :].bitcast(I32), picked_scales[8 * i:P:32, :].bitcast(I32))
 
-        fp4 = keep.tile([P, 6 * N], U8, name="fp4", tag="scale_slot", align_bytes=64)
-        nc.vector.memset(fp4[:, :2 * N].bitcast(I32), 0)
-        w1_plane, w3_plane = fp4[:, :N], fp4[:, N:2 * N]
-        w1_codes, w3_codes = fp4[:, 2 * N:4 * N], fp4[:, 4 * N:]
+        w2_bf = keep.tile([P, PACK * H], BF16, name="w2_bf", align_bytes=64)
+        src = w2_raw[:].rearrange("p j (m t) -> p m t j", t=PACK)
+        dst = w2_bf[:].rearrange("p (t m j) -> p m t j", t=PACK, j=PACK)
+        nc.vector.tensor_copy(dst[:, :M_VECTOR], src[:, :M_VECTOR])
+        nc.scalar.copy(dst[:, M_VECTOR:], src[:, M_VECTOR:])
+        fp4 = keep.tile([P, 6 * N + WARM_M], U8, name="fp4", tag="raw_slot", align_bytes=64)
+        nc.vector.memset(fp4[:, :2 * N + WARM_M].bitcast(I32), 0)
+        w1_plane, w3_plane, warm_plane = fp4[:, :N], fp4[:, N:2 * N], fp4[:, 2 * N:2 * N + WARM_M]
+        w1_codes, w3_codes = fp4[:, 2 * N + WARM_M:4 * N + WARM_M], fp4[:, 4 * N + WARM_M:]
         nc.sync.dma_start(w1_codes.bitcast(I32), w1_words[0].bitcast(I32))
         nc.sync.dma_start(w3_codes.bitcast(I32), w3_words[0].bitcast(I32))
         for plane, rows in ((w1_plane, w1_scales), (w3_plane, w3_scales)):
             for i in range(4):
                 nc.sync.dma_start(plane[i:P:32, :].bitcast(I32), rows[0, i:16:4, :].bitcast(I32))
 
-        w2_bf = keep.tile([P, PACK * H], BF16, name="w2_bf", align_bytes=64)
-        src = w2_raw[:].rearrange("p j (m t) -> p m t j", t=PACK)
-        dst = w2_bf[:].rearrange("p (t m j) -> p m t j", t=PACK, j=PACK)
-        nc.vector.tensor_copy(dst[:, :M_VECTOR], src[:, :M_VECTOR])
-        nc.scalar.copy(dst[:, M_VECTOR:], src[:, M_VECTOR:])
+        warm_bank = psum.tile([P, S], F32, name="warm_bank", tag="last_bank")
+        for rep in range(2):
+            nc.tensor.matmul_mx(out=warm_bank[:WARM_M, :], lhsT=h_codes_all[:, :WARM_M].bitcast(FP8X4), lhsT_scale=warm_plane,
+                                rhs=h_codes_all[:].bitcast(FP8X4), rhs_scale=picked_scales[:], start=True, stop=True)
+
         w2_codes = keep.tile([P, H], U32, name="w2_codes", align_bytes=64)
         w2_plane = keep.tile([P, H], U8, name="w2_plane", align_bytes=64)
         nc.vector.quantize_mx(out=w2_codes[:].bitcast(FP8X4), scales=w2_plane[:], in_=w2_bf[:])
@@ -101,15 +109,15 @@ def tile_picked_phlora_gelu_p_kernel(tc, x_words, x_scales, w1_words, w1_scales,
 
         for c in range(S // CHUNK):
             x_codes, x_bytes = x_operand(c)
-            h_codes = keep.tile([P, CHUNK], U32, name=f"h_codes{c}", align_bytes=64)
+            h_codes = h_codes_all[:, c * CHUNK:(c + 1) * CHUNK]
             h_plane = keep.tile([P, CHUNK], U8, name=f"h_plane{c}", align_bytes=64)
             for part in parts(c):
                 nc.vector.quantize_mx(out=h_codes[:, part].bitcast(FP8X4), scales=h_plane[:, part], in_=hidden[c][:, PACK * part.start:PACK * part.stop])
-            acc = psum.tile([P, CHUNK], F32, name=f"acc{c}")
+            acc = psum.tile([P, CHUNK], F32, name=f"acc{c}", tag="last_bank" if c == S // CHUNK - 1 else f"acc{c}")
             nc.tensor.matmul_mx(out=acc[:], lhsT=w1_codes.bitcast(FP4X4), lhsT_scale=w1_plane,
                                 rhs=x_codes, rhs_scale=x_bytes, start=True, stop=False)
             nc.tensor.matmul_mx(out=acc[:], lhsT=w3_codes.bitcast(FP4X4), lhsT_scale=w3_plane,
-                                rhs=h_codes[:].bitcast(FP8X4), rhs_scale=h_plane[:], start=False, stop=True)
+                                rhs=h_codes.bitcast(FP8X4), rhs_scale=h_plane[:], start=False, stop=True)
             result = keep.tile([P, CHUNK], F32, name=f"result{c}", align_bytes=64)
             if c < 2:
                 nc.scalar.copy(result[:], acc[:])

@@ -30,14 +30,12 @@ def tile_picked_phlora_gelu_p_kernel(tc, x_words, x_scales, w1_words, w1_scales,
 
         scale_table = keep.tile([P, T], U8, name="scale_table", align_bytes=64)
         nc.vector.memset(scale_table[:].bitcast(I32), 0)
-        warm_in = keep.tile([P, 1], F32, name="warm_in")
-        nc.vector.memset(warm_in[:], 0.0)
-        warm_out = keep.tile([P, 1], F32, name="warm_out")
-        nc.scalar.activation(warm_out[:], warm_in[:], GELU)
         x_plane = keep.tile([P, S], U8, name="x_plane", align_bytes=64)
         nc.vector.memset(x_plane[:].bitcast(I32), 0)
         h_codes_all = keep.tile([P, S], U32, name="h_codes_all", align_bytes=64)
         nc.vector.memset(h_codes_all[:].bitcast(I32), 0)
+        warm_out = keep.tile([P, 1], F32, name="warm_out")
+        nc.scalar.activation(warm_out[:], h_codes_all[:, :1].bitcast(F32), GELU)
 
         w2_raw = keep.tile([P, PACK, H], F32, name="w2_raw", tag="raw_slot", align_bytes=64)
         w2_rows = w2.rearrange("(p j) c -> p j c", j=PACK)
@@ -119,8 +117,5 @@ def tile_picked_phlora_gelu_p_kernel(tc, x_words, x_scales, w1_words, w1_scales,
             nc.tensor.matmul_mx(out=acc[:], lhsT=w3_codes.bitcast(FP4X4), lhsT_scale=w3_plane,
                                 rhs=h_codes.bitcast(FP8X4), rhs_scale=h_plane[:], start=False, stop=True)
             result = keep.tile([P, CHUNK], F32, name=f"result{c}", align_bytes=64)
-            if c < 2:
-                nc.scalar.copy(result[:], acc[:])
-            else:
-                nc.vector.tensor_copy(result[:], acc[:])
+            nc.scalar.copy(result[:], acc[:])
             nc.sync.dma_start(out[:, c * CHUNK:(c + 1) * CHUNK], result[:])

@@ -15,15 +15,22 @@ GELU = mybir.ActivationFunctionType.Gelu_apprx_tanh
 P = 128
 K, T, S, H, N = 512, 2048, 512, 512, 128
 PACK = 4
+BLOCK_ROWS = 8
+QUADRANT = 32
+LIST_ROWS = 16
 CHUNK = 128
-HALF = 256
-M_VECTOR = 88
+GATHER = 256
+VECTOR_GROUPS = 88
+WARM_GROUPS = 32
+WARM_AFTER = 48
 WARM_M = 64
+WARM_PASSES = 2
 FLOPS = 2 * S * (K * H + K * N + H * N)
 
 
 def tile_picked_phlora_gelu_p_kernel(tc, x_words, x_scales, w1_words, w1_scales, w2, w3_words, w3_scales, offs, out):
     nc = tc.nc
+    chunks = S // CHUNK
     with ExitStack() as ctx:
         keep = ctx.enter_context(tc.tile_pool(name="keep", bufs=1))
         psum = ctx.enter_context(tc.psum_pool(name="psum", bufs=1))
@@ -32,17 +39,23 @@ def tile_picked_phlora_gelu_p_kernel(tc, x_words, x_scales, w1_words, w1_scales,
         nc.vector.memset(scale_table[:].bitcast(I32), 0)
         x_plane = keep.tile([P, S], U8, name="x_plane", align_bytes=64)
         nc.vector.memset(x_plane[:].bitcast(I32), 0)
-        h_codes_all = keep.tile([P, S], U32, name="h_codes_all", align_bytes=64)
-        nc.vector.memset(h_codes_all[:].bitcast(I32), 0)
-        warm_out = keep.tile([P, 1], F32, name="warm_out")
-        nc.scalar.activation(warm_out[:], h_codes_all[:, :1].bitcast(F32), GELU)
 
-        w2_raw = keep.tile([P, PACK, H], F32, name="w2_raw", tag="raw_slot", align_bytes=64)
+        second = keep.tile([P, 6 * N + WARM_M + PACK * S], U8, name="second", align_bytes=64)
+        zeroed = 2 * N + WARM_M + PACK * S
+        nc.vector.memset(second[:, :zeroed].bitcast(I32), 0)
+        w1_plane, w3_plane, warm_plane = second[:, :N], second[:, N:2 * N], second[:, 2 * N:2 * N + WARM_M]
+        h_codes = second[:, 2 * N + WARM_M:zeroed].bitcast(U32)
+        w1_codes, w3_codes = second[:, zeroed:zeroed + 2 * N], second[:, zeroed + 2 * N:]
+
+        warm_column = keep.tile([P, 1], F32, name="warm_column")
+        nc.scalar.activation(warm_column[:], h_codes[:, :1].bitcast(F32), GELU)
+
+        w2_raw = keep.tile([P, PACK, H], F32, name="w2_raw", align_bytes=64)
         w2_rows = w2.rearrange("(p j) c -> p j c", j=PACK)
         nc.sync.dma_start(w2_raw[:, :1], w2_rows[:, :1])
-        offsets = keep.tile([P, S // 16], U16, name="offsets")
+        offsets = keep.tile([P, S // LIST_ROWS], U16, name="offsets")
         nc.sync.dma_start(offsets[:], offs)
-        nc.sync.dma_start(scale_table[0:P:8, :].bitcast(I32), x_scales[0].bitcast(I32))
+        nc.sync.dma_start(scale_table[0:P:BLOCK_ROWS, :].bitcast(I32), x_scales[0].bitcast(I32))
         nc.sync.dma_start(w2_raw[:, 1:], w2_rows[:, 1:])
 
         word_table = keep.tile([P, T], I32, name="word_table", align_bytes=64)
@@ -50,50 +63,52 @@ def tile_picked_phlora_gelu_p_kernel(tc, x_words, x_scales, w1_words, w1_scales,
 
         picked_scales = keep.tile([P, S], U8, name="picked_scales", align_bytes=64)
         nc.vector.tensor_copy(picked_scales[:], scale_table[:].indirect(offsets[:]))
-        for i in range(4):
-            nc.sync.dma_start(x_plane[i:P:32, :].bitcast(I32), picked_scales[8 * i:P:32, :].bitcast(I32))
+        rows_in_quadrant = QUADRANT // BLOCK_ROWS
+        for i in range(rows_in_quadrant):
+            nc.sync.dma_start(x_plane[i:P:QUADRANT, :].bitcast(I32), picked_scales[BLOCK_ROWS * i:P:QUADRANT, :].bitcast(I32))
+
+        nc.sync.dma_start(w1_codes.bitcast(I32), w1_words[0].bitcast(I32))
+        nc.sync.dma_start(w3_codes.bitcast(I32), w3_words[0].bitcast(I32))
+        for plane, rows in ((w1_plane, w1_scales), (w3_plane, w3_scales)):
+            for i in range(rows_in_quadrant):
+                nc.sync.dma_start(plane[i:P:QUADRANT, :].bitcast(I32), rows[0, i::rows_in_quadrant, :].bitcast(I32))
 
         w2_bf = keep.tile([P, PACK * H], BF16, name="w2_bf", align_bytes=64)
         src = w2_raw[:].rearrange("p j (m t) -> p m t j", t=PACK)
         dst = w2_bf[:].rearrange("p (t m j) -> p m t j", t=PACK, j=PACK)
-        nc.vector.tensor_copy(dst[:, :M_VECTOR], src[:, :M_VECTOR])
-        nc.scalar.copy(dst[:, M_VECTOR:], src[:, M_VECTOR:])
-        fp4 = keep.tile([P, 6 * N + WARM_M], U8, name="fp4", tag="raw_slot", align_bytes=64)
-        nc.vector.memset(fp4[:, :2 * N + WARM_M].bitcast(I32), 0)
-        w1_plane, w3_plane, warm_plane = fp4[:, :N], fp4[:, N:2 * N], fp4[:, 2 * N:2 * N + WARM_M]
-        w1_codes, w3_codes = fp4[:, 2 * N + WARM_M:4 * N + WARM_M], fp4[:, 4 * N + WARM_M:]
-        nc.sync.dma_start(w1_codes.bitcast(I32), w1_words[0].bitcast(I32))
-        nc.sync.dma_start(w3_codes.bitcast(I32), w3_words[0].bitcast(I32))
-        for plane, rows in ((w1_plane, w1_scales), (w3_plane, w3_scales)):
-            for i in range(4):
-                nc.sync.dma_start(plane[i:P:32, :].bitcast(I32), rows[0, i:16:4, :].bitcast(I32))
+        nc.vector.tensor_copy(dst[:, :WARM_GROUPS], src[:, :WARM_GROUPS])
+        nc.vector.tensor_copy(dst[:, WARM_GROUPS:WARM_AFTER], src[:, WARM_GROUPS:WARM_AFTER])
+        nc.vector.quantize_mx(out=h_codes[:, :WARM_GROUPS].bitcast(FP8X4), scales=warm_plane[:, :WARM_GROUPS], in_=w2_bf[:, :PACK * WARM_GROUPS])
+        nc.vector.tensor_copy(dst[:, WARM_AFTER:VECTOR_GROUPS], src[:, WARM_AFTER:VECTOR_GROUPS])
+        nc.scalar.copy(dst[:, VECTOR_GROUPS:], src[:, VECTOR_GROUPS:])
 
         warm_bank = psum.tile([P, S], F32, name="warm_bank", tag="last_bank")
-        for rep in range(2):
-            nc.tensor.matmul_mx(out=warm_bank[:WARM_M, :], lhsT=h_codes_all[:, :WARM_M].bitcast(FP8X4), lhsT_scale=warm_plane,
-                                rhs=h_codes_all[:].bitcast(FP8X4), rhs_scale=picked_scales[:], start=True, stop=True)
+        for warm_pass in range(WARM_PASSES):
+            nc.tensor.matmul_mx(out=warm_bank[:WARM_M, :], lhsT=h_codes[:, :WARM_M].bitcast(FP8X4), lhsT_scale=warm_plane,
+                                rhs=h_codes.bitcast(FP8X4), rhs_scale=picked_scales[:], start=True, stop=True)
 
         w2_codes = keep.tile([P, H], U32, name="w2_codes", align_bytes=64)
         w2_plane = keep.tile([P, H], U8, name="w2_plane", align_bytes=64)
         nc.vector.quantize_mx(out=w2_codes[:].bitcast(FP8X4), scales=w2_plane[:], in_=w2_bf[:])
 
         picked_words = []
-        for u in range(S // HALF):
-            words = keep.tile([P, HALF], U32, name=f"picked_words{u}", align_bytes=64)
-            nc.vector.tensor_copy(words[:], word_table[:].bitcast(U32).indirect(offsets[:, u * HALF // 16:(u + 1) * HALF // 16]))
+        for u in range(S // GATHER):
+            words = keep.tile([P, GATHER], U32, name=f"picked_words{u}", align_bytes=64)
+            entries = offsets[:, u * GATHER // LIST_ROWS:(u + 1) * GATHER // LIST_ROWS]
+            nc.vector.tensor_copy(words[:], word_table[:].bitcast(U32).indirect(entries))
             picked_words.append(words)
 
         def x_operand(c):
-            u, lo = divmod(c * CHUNK, HALF)
+            u, lo = divmod(c * CHUNK, GATHER)
             return picked_words[u][:, lo:lo + CHUNK].bitcast(FP8X4), x_plane[:, c * CHUNK:(c + 1) * CHUNK]
 
         def parts(c):
-            if c == S // CHUNK - 1:
+            if c == chunks - 1:
                 return [slice(0, CHUNK // 2), slice(CHUNK // 2, CHUNK)]
             return [slice(0, CHUNK)]
 
         hidden = []
-        for c in range(S // CHUNK):
+        for c in range(chunks):
             x_codes, x_bytes = x_operand(c)
             pre = psum.tile([P, PACK, CHUNK], F32, name=f"pre{c}")
             for t in range(PACK):
@@ -105,17 +120,17 @@ def tile_picked_phlora_gelu_p_kernel(tc, x_words, x_scales, w1_words, w1_scales,
                 nc.scalar.activation(h[:].rearrange("p (n t) -> p n t", t=PACK)[:, part], pre[:].rearrange("p t n -> p n t")[:, part], GELU)
             hidden.append(h)
 
-        for c in range(S // CHUNK):
+        for c in range(chunks):
             x_codes, x_bytes = x_operand(c)
-            h_codes = h_codes_all[:, c * CHUNK:(c + 1) * CHUNK]
+            chunk_codes = h_codes[:, c * CHUNK:(c + 1) * CHUNK]
             h_plane = keep.tile([P, CHUNK], U8, name=f"h_plane{c}", align_bytes=64)
             for part in parts(c):
-                nc.vector.quantize_mx(out=h_codes[:, part].bitcast(FP8X4), scales=h_plane[:, part], in_=hidden[c][:, PACK * part.start:PACK * part.stop])
-            acc = psum.tile([P, CHUNK], F32, name=f"acc{c}", tag="last_bank" if c == S // CHUNK - 1 else f"acc{c}")
+                nc.vector.quantize_mx(out=chunk_codes[:, part].bitcast(FP8X4), scales=h_plane[:, part], in_=hidden[c][:, PACK * part.start:PACK * part.stop])
+            acc = psum.tile([P, CHUNK], F32, name=f"acc{c}", tag="last_bank" if c == chunks - 1 else f"acc{c}")
             nc.tensor.matmul_mx(out=acc[:], lhsT=w1_codes.bitcast(FP4X4), lhsT_scale=w1_plane,
                                 rhs=x_codes, rhs_scale=x_bytes, start=True, stop=False)
             nc.tensor.matmul_mx(out=acc[:], lhsT=w3_codes.bitcast(FP4X4), lhsT_scale=w3_plane,
-                                rhs=h_codes.bitcast(FP8X4), rhs_scale=h_plane[:], start=False, stop=True)
+                                rhs=chunk_codes.bitcast(FP8X4), rhs_scale=h_plane[:], start=False, stop=True)
             result = keep.tile([P, CHUNK], F32, name=f"result{c}", align_bytes=64)
             nc.scalar.copy(result[:], acc[:])
             nc.sync.dma_start(out[:, c * CHUNK:(c + 1) * CHUNK], result[:])

@@ -25,6 +25,8 @@ WARM_GROUPS = 32
 WARM_AFTER = 48
 WARM_M = 64
 WARM_PASSES = 2
+PAIRED = 2
+ACC_TAGS = ["pair0_0", "pair0_1", "acc2"]
 FLOPS = 2 * S * (K * H + K * N + H * N)
 
 
@@ -107,17 +109,29 @@ def tile_picked_phlora_gelu_p_kernel(tc, x_words, x_scales, w1_words, w1_scales,
                 return [slice(0, CHUNK // 2), slice(CHUNK // 2, CHUNK)]
             return [slice(0, CHUNK)]
 
+        def first_pass(bank, c, t):
+            x_codes, x_bytes = x_operand(c)
+            cols = slice(t * P, (t + 1) * P)
+            nc.tensor.matmul_mx(out=bank, lhsT=w2_codes[:, cols].bitcast(FP8X4), lhsT_scale=w2_plane[:, cols],
+                                rhs=x_codes, rhs_scale=x_bytes, start=True, stop=True)
+
         hidden = []
         for c in range(chunks):
-            x_codes, x_bytes = x_operand(c)
-            pre = psum.tile([P, PACK, CHUNK], F32, name=f"pre{c}")
-            for t in range(PACK):
-                cols = slice(t * P, (t + 1) * P)
-                nc.tensor.matmul_mx(out=pre[:, t, :], lhsT=w2_codes[:, cols].bitcast(FP8X4), lhsT_scale=w2_plane[:, cols],
-                                    rhs=x_codes, rhs_scale=x_bytes, start=True, stop=True)
             h = keep.tile([P, CHUNK * PACK], BF16, name=f"h{c}", align_bytes=64)
-            for part in parts(c):
-                nc.scalar.activation(h[:].rearrange("p (n t) -> p n t", t=PACK)[:, part], pre[:].rearrange("p t n -> p n t")[:, part], GELU)
+            if c < PAIRED:
+                pairs = keep.tile([P, 2, 2 * CHUNK], BF16, name=f"pairs{c}", align_bytes=64)
+                for u in range(2):
+                    pre = psum.tile([P, 2, CHUNK], F32, name=f"pre{c}_{u}", tag=f"pair{c}_{u}")
+                    for e in range(2):
+                        first_pass(pre[:, e, :], c, 2 * u + e)
+                    nc.scalar.activation(pairs[:, u, :].rearrange("p (n e) -> p n e", e=2), pre[:].rearrange("p e n -> p n e"), GELU)
+                nc.vector.tensor_copy(h[:].bitcast(I32).rearrange("p (n u) -> p n u", u=2), pairs[:].bitcast(I32).rearrange("p u n -> p n u"))
+            else:
+                pre = psum.tile([P, PACK, CHUNK], F32, name=f"pre{c}")
+                for t in range(PACK):
+                    first_pass(pre[:, t, :], c, t)
+                for part in parts(c):
+                    nc.scalar.activation(h[:].rearrange("p (n t) -> p n t", t=PACK)[:, part], pre[:].rearrange("p t n -> p n t")[:, part], GELU)
             hidden.append(h)
 
         for c in range(chunks):
@@ -126,7 +140,7 @@ def tile_picked_phlora_gelu_p_kernel(tc, x_words, x_scales, w1_words, w1_scales,
             h_plane = keep.tile([P, CHUNK], U8, name=f"h_plane{c}", align_bytes=64)
             for part in parts(c):
                 nc.vector.quantize_mx(out=chunk_codes[:, part].bitcast(FP8X4), scales=h_plane[:, part], in_=hidden[c][:, PACK * part.start:PACK * part.stop])
-            acc = psum.tile([P, CHUNK], F32, name=f"acc{c}", tag="last_bank" if c == chunks - 1 else f"acc{c}")
+            acc = psum.tile([P, CHUNK], F32, name=f"acc{c}", tag="last_bank" if c == chunks - 1 else ACC_TAGS[c])
             nc.tensor.matmul_mx(out=acc[:], lhsT=w1_codes.bitcast(FP4X4), lhsT_scale=w1_plane,
                                 rhs=x_codes, rhs_scale=x_bytes, start=True, stop=False)
             nc.tensor.matmul_mx(out=acc[:], lhsT=w3_codes.bitcast(FP4X4), lhsT_scale=w3_plane,

@@ -20,9 +20,7 @@ QUADRANT = 32
 LIST_ROWS = 16
 CHUNK = 128
 GATHER = 256
-VECTOR_GROUPS = 88
-WARM_GROUPS = 32
-WARM_AFTER = 48
+VECTOR_GROUPS = 80
 WARM_M = 64
 WARM_PASSES = 2
 PAIRED = 2
@@ -42,15 +40,12 @@ def tile_picked_phlora_gelu_p_kernel(tc, x_words, x_scales, w1_words, w1_scales,
         x_plane = keep.tile([P, S], U8, name="x_plane", align_bytes=64)
         nc.vector.memset(x_plane[:].bitcast(I32), 0)
 
-        second = keep.tile([P, 6 * N + WARM_M + PACK * S], U8, name="second", align_bytes=64)
-        zeroed = 2 * N + WARM_M + PACK * S
-        nc.vector.memset(second[:, :zeroed].bitcast(I32), 0)
-        w1_plane, w3_plane, warm_plane = second[:, :N], second[:, N:2 * N], second[:, 2 * N:2 * N + WARM_M]
-        h_codes = second[:, 2 * N + WARM_M:zeroed].bitcast(U32)
-        w1_codes, w3_codes = second[:, zeroed:zeroed + 2 * N], second[:, zeroed + 2 * N:]
+        fp4 = keep.tile([P, 6 * N], U8, name="fp4", align_bytes=64)
+        nc.vector.memset(fp4[:, :2 * N].bitcast(I32), 0)
+        w1_plane, w3_plane, w1_codes, w3_codes = fp4[:, :N], fp4[:, N:2 * N], fp4[:, 2 * N:4 * N], fp4[:, 4 * N:]
 
         warm_column = keep.tile([P, 1], F32, name="warm_column")
-        nc.scalar.activation(warm_column[:], h_codes[:, :1].bitcast(F32), GELU)
+        nc.scalar.activation(warm_column[:], w1_plane[:, :4].bitcast(F32), GELU)
 
         w2_raw = keep.tile([P, PACK, H], F32, name="w2_raw", align_bytes=64)
         w2_rows = w2.rearrange("(p j) c -> p j c", j=PACK)
@@ -78,20 +73,16 @@ def tile_picked_phlora_gelu_p_kernel(tc, x_words, x_scales, w1_words, w1_scales,
         w2_bf = keep.tile([P, PACK * H], BF16, name="w2_bf", align_bytes=64)
         src = w2_raw[:].rearrange("p j (m t) -> p m t j", t=PACK)
         dst = w2_bf[:].rearrange("p (t m j) -> p m t j", t=PACK, j=PACK)
-        nc.vector.tensor_copy(dst[:, :WARM_GROUPS], src[:, :WARM_GROUPS])
-        nc.vector.tensor_copy(dst[:, WARM_GROUPS:WARM_AFTER], src[:, WARM_GROUPS:WARM_AFTER])
-        nc.vector.quantize_mx(out=h_codes[:, :WARM_GROUPS].bitcast(FP8X4), scales=warm_plane[:, :WARM_GROUPS], in_=w2_bf[:, :PACK * WARM_GROUPS])
-        nc.vector.tensor_copy(dst[:, WARM_AFTER:VECTOR_GROUPS], src[:, WARM_AFTER:VECTOR_GROUPS])
+        nc.vector.tensor_copy(dst[:, :VECTOR_GROUPS], src[:, :VECTOR_GROUPS])
         nc.scalar.copy(dst[:, VECTOR_GROUPS:], src[:, VECTOR_GROUPS:])
-
-        warm_bank = psum.tile([P, S], F32, name="warm_bank", tag="last_bank")
-        for warm_pass in range(WARM_PASSES):
-            nc.tensor.matmul_mx(out=warm_bank[:WARM_M, :], lhsT=h_codes[:, :WARM_M].bitcast(FP8X4), lhsT_scale=warm_plane,
-                                rhs=h_codes.bitcast(FP8X4), rhs_scale=picked_scales[:], start=True, stop=True)
-
         w2_codes = keep.tile([P, H], U32, name="w2_codes", align_bytes=64)
         w2_plane = keep.tile([P, H], U8, name="w2_plane", align_bytes=64)
         nc.vector.quantize_mx(out=w2_codes[:].bitcast(FP8X4), scales=w2_plane[:], in_=w2_bf[:])
+
+        warm_bank = psum.tile([P, S], F32, name="warm_bank", tag="last_bank")
+        for warm_pass in range(WARM_PASSES):
+            nc.tensor.matmul_mx(out=warm_bank[:WARM_M, :], lhsT=w2_codes[:, :WARM_M].bitcast(FP8X4), lhsT_scale=w2_plane[:, :WARM_M],
+                                rhs=w2_codes[:].bitcast(FP8X4), rhs_scale=w2_plane[:], start=True, stop=True)
 
         picked_words = []
         for u in range(S // GATHER):
@@ -136,7 +127,7 @@ def tile_picked_phlora_gelu_p_kernel(tc, x_words, x_scales, w1_words, w1_scales,
 
         for c in range(chunks):
             x_codes, x_bytes = x_operand(c)
-            chunk_codes = h_codes[:, c * CHUNK:(c + 1) * CHUNK]
+            chunk_codes = keep.tile([P, CHUNK], U32, name=f"h_codes{c}", align_bytes=64)
             h_plane = keep.tile([P, CHUNK], U8, name=f"h_plane{c}", align_bytes=64)
             for part in parts(c):
                 nc.vector.quantize_mx(out=chunk_codes[:, part].bitcast(FP8X4), scales=h_plane[:, part], in_=hidden[c][:, PACK * part.start:PACK * part.stop])
@@ -144,7 +135,10 @@ def tile_picked_phlora_gelu_p_kernel(tc, x_words, x_scales, w1_words, w1_scales,
             nc.tensor.matmul_mx(out=acc[:], lhsT=w1_codes.bitcast(FP4X4), lhsT_scale=w1_plane,
                                 rhs=x_codes, rhs_scale=x_bytes, start=True, stop=False)
             nc.tensor.matmul_mx(out=acc[:], lhsT=w3_codes.bitcast(FP4X4), lhsT_scale=w3_plane,
-                                rhs=chunk_codes.bitcast(FP8X4), rhs_scale=h_plane[:], start=False, stop=True)
+                                rhs=chunk_codes[:].bitcast(FP8X4), rhs_scale=h_plane[:], start=False, stop=True)
             result = keep.tile([P, CHUNK], F32, name=f"result{c}", align_bytes=64)
-            nc.scalar.copy(result[:], acc[:])
+            if c == chunks - 1:
+                nc.vector.tensor_copy(result[:], acc[:])
+            else:
+                nc.scalar.copy(result[:], acc[:])
             nc.sync.dma_start(out[:, c * CHUNK:(c + 1) * CHUNK], result[:])

@@ -20,9 +20,8 @@ QUADRANT = 32
 LIST_ROWS = 16
 CHUNK = 128
 GATHER = 256
-VECTOR_GROUPS = 80
-WARM_M = 64
-WARM_PASSES = 2
+VECTOR_GROUPS = 78
+WARM_PASSES = ((64, 512), (128, 256))
 PAIRED = 2
 ACC_TAGS = ["pair0_0", "pair0_1", "acc2"]
 FLOPS = 2 * S * (K * H + K * N + H * N)
@@ -80,9 +79,9 @@ def tile_picked_phlora_gelu_p_kernel(tc, x_words, x_scales, w1_words, w1_scales,
         nc.vector.quantize_mx(out=w2_codes[:].bitcast(FP8X4), scales=w2_plane[:], in_=w2_bf[:])
 
         warm_bank = psum.tile([P, S], F32, name="warm_bank", tag="last_bank")
-        for warm_pass in range(WARM_PASSES):
-            nc.tensor.matmul_mx(out=warm_bank[:WARM_M, :], lhsT=w2_codes[:, :WARM_M].bitcast(FP8X4), lhsT_scale=w2_plane[:, :WARM_M],
-                                rhs=w2_codes[:].bitcast(FP8X4), rhs_scale=w2_plane[:], start=True, stop=True)
+        for rows, width in WARM_PASSES:
+            nc.tensor.matmul_mx(out=warm_bank[:rows, :width], lhsT=w2_codes[:, :rows].bitcast(FP8X4), lhsT_scale=w2_plane[:, :rows],
+                                rhs=w2_codes[:, :width].bitcast(FP8X4), rhs_scale=w2_plane[:, :width], start=True, stop=True)
 
         picked_words = []
         for u in range(S // GATHER):

@@ -21,7 +21,7 @@ LIST_ROWS = 16
 CHUNK = 128
 GATHER = 256
 VECTOR_GROUPS = 78
-WARM_PASSES = ((64, 512), (128, 256))
+WARM_PASSES = ((32, 128), (32, 128), (32, 128), (32, 128), (32, 512))
 PAIRED = 2
 ACC_TAGS = ["pair0_0", "pair0_1", "acc2"]
 FLOPS = 2 * S * (K * H + K * N + H * N)
@@ -76,7 +76,8 @@ def tile_picked_phlora_gelu_p_kernel(tc, x_words, x_scales, w1_words, w1_scales,
         nc.scalar.copy(dst[:, VECTOR_GROUPS:], src[:, VECTOR_GROUPS:])
         w2_codes = keep.tile([P, H], U32, name="w2_codes", align_bytes=64)
         w2_plane = keep.tile([P, H], U8, name="w2_plane", align_bytes=64)
-        nc.vector.quantize_mx(out=w2_codes[:].bitcast(FP8X4), scales=w2_plane[:], in_=w2_bf[:])
+        for cols in (slice(0, P), slice(P, 2 * P), slice(2 * P, H)):
+            nc.vector.quantize_mx(out=w2_codes[:, cols].bitcast(FP8X4), scales=w2_plane[:, cols], in_=w2_bf[:, PACK * cols.start:PACK * cols.stop])
 
         warm_bank = psum.tile([P, S], F32, name="warm_bank", tag="last_bank")
         for rows, width in WARM_PASSES:

@@ -22,8 +22,8 @@ CHUNK = 128
 GATHER = 256
 VECTOR_GROUPS = 78
 WARM_PASSES = ((32, 128), (32, 128), (32, 128), (32, 128), (32, 512))
-PAIRED = 2
-ACC_TAGS = ["pair0_0", "pair0_1", "acc2"]
+FIRST_GROUPS = ((0, 1), (1, 2), (2, 4))
+ACC_TAGS = ("bank0_0", "bank0_1", "acc2", "acc3")
 FLOPS = 2 * S * (K * H + K * N + H * N)
 
 
@@ -109,16 +109,16 @@ def tile_picked_phlora_gelu_p_kernel(tc, x_words, x_scales, w1_words, w1_scales,
         hidden = []
         for c in range(chunks):
             h = keep.tile([P, CHUNK * PACK], BF16, name=f"h{c}", align_bytes=64)
-            if c < PAIRED:
-                pairs = keep.tile([P, 2, 2 * CHUNK], BF16, name=f"pairs{c}", align_bytes=64)
-                for u in range(2):
-                    pre = psum.tile([P, 2, CHUNK], F32, name=f"pre{c}_{u}", tag=f"pair{c}_{u}")
-                    for e in range(2):
-                        first_pass(pre[:, e, :], c, 2 * u + e)
-                    nc.scalar.activation(pairs[:, u, :].rearrange("p (n e) -> p n e", e=2), pre[:].rearrange("p e n -> p n e"), GELU)
-                nc.vector.tensor_copy(h[:].bitcast(I32).rearrange("p (n u) -> p n u", u=2), pairs[:].bitcast(I32).rearrange("p u n -> p n u"))
+            if c == 0:
+                loose = keep.tile([P, PACK, CHUNK], BF16, name="loose", align_bytes=64)
+                for u, (lo, hi) in enumerate(FIRST_GROUPS):
+                    pre = psum.tile([P, hi - lo, CHUNK], F32, name=f"pre0_{u}", tag=f"bank0_{u}")
+                    for t in range(lo, hi):
+                        first_pass(pre[:, t - lo, :], c, t)
+                    nc.scalar.activation(loose[:, lo:hi, :], pre[:], GELU)
+                nc.vector.tensor_copy(h[:].rearrange("p (n u) -> p n u", u=PACK), loose[:].rearrange("p u n -> p n u"))
             else:
-                pre = psum.tile([P, PACK, CHUNK], F32, name=f"pre{c}")
+                pre = psum.tile([P, PACK, CHUNK], F32, name=f"pre{c}", tag="last_bank" if c == chunks - 1 else f"whole{c}")
                 for t in range(PACK):
                     first_pass(pre[:, t, :], c, t)
                 for part in parts(c):
@@ -131,7 +131,7 @@ def tile_picked_phlora_gelu_p_kernel(tc, x_words, x_scales, w1_words, w1_scales,
             h_plane = keep.tile([P, CHUNK], U8, name=f"h_plane{c}", align_bytes=64)
             for part in parts(c):
                 nc.vector.quantize_mx(out=chunk_codes[:, part].bitcast(FP8X4), scales=h_plane[:, part], in_=hidden[c][:, PACK * part.start:PACK * part.stop])
-            acc = psum.tile([P, CHUNK], F32, name=f"acc{c}", tag="last_bank" if c == chunks - 1 else ACC_TAGS[c])
+            acc = psum.tile([P, CHUNK], F32, name=f"acc{c}", tag=ACC_TAGS[c])
             nc.tensor.matmul_mx(out=acc[:], lhsT=w1_codes.bitcast(FP4X4), lhsT_scale=w1_plane,
                                 rhs=x_codes, rhs_scale=x_bytes, start=True, stop=False)
             nc.tensor.matmul_mx(out=acc[:], lhsT=w3_codes.bitcast(FP4X4), lhsT_scale=w3_plane,

@@ -72,8 +72,9 @@ def tile_picked_phlora_gelu_p_kernel(tc, x_words, x_scales, w1_words, w1_scales,
         w2_bf = keep.tile([P, PACK * H], BF16, name="w2_bf", align_bytes=64)
         src = w2_raw[:].rearrange("p j (m t) -> p m t j", t=PACK)
         dst = w2_bf[:].rearrange("p (t m j) -> p m t j", t=PACK, j=PACK)
-        nc.vector.tensor_copy(dst[:, :VECTOR_GROUPS], src[:, :VECTOR_GROUPS])
-        nc.scalar.copy(dst[:, VECTOR_GROUPS:], src[:, VECTOR_GROUPS:])
+        for rows in (slice(0, 1), slice(1, PACK)):
+            nc.vector.tensor_copy(dst[:, :VECTOR_GROUPS, :, rows], src[:, :VECTOR_GROUPS, :, rows])
+            nc.scalar.copy(dst[:, VECTOR_GROUPS:, :, rows], src[:, VECTOR_GROUPS:, :, rows])
         w2_codes = keep.tile([P, H], U32, name="w2_codes", align_bytes=64)
         w2_plane = keep.tile([P, H], U8, name="w2_plane", align_bytes=64)
         for cols in (slice(0, P), slice(P, 2 * P), slice(2 * P, H)):

@@ -52,7 +52,8 @@ def tile_picked_phlora_gelu_p_kernel(tc, x_words, x_scales, w1_words, w1_scales,
         offsets = keep.tile([P, S // LIST_ROWS], U16, name="offsets")
         nc.sync.dma_start(offsets[:], offs)
         nc.sync.dma_start(scale_table[0:P:BLOCK_ROWS, :].bitcast(I32), x_scales[0].bitcast(I32))
-        nc.sync.dma_start(w2_raw[:, 1:], w2_rows[:, 1:])
+        nc.sync.dma_start(w2_raw[:, 1:2], w2_rows[:, 1:2])
+        nc.sync.dma_start(w2_raw[:, 2:], w2_rows[:, 2:])
 
         word_table = keep.tile([P, T], I32, name="word_table", align_bytes=64)
         nc.sync.dma_start(word_table[:], x_words[0].rearrange("p n t -> p (n t)").bitcast(I32))
@@ -72,7 +73,7 @@ def tile_picked_phlora_gelu_p_kernel(tc, x_words, x_scales, w1_words, w1_scales,
         w2_bf = keep.tile([P, PACK * H], BF16, name="w2_bf", align_bytes=64)
         src = w2_raw[:].rearrange("p j (m t) -> p m t j", t=PACK)
         dst = w2_bf[:].rearrange("p (t m j) -> p m t j", t=PACK, j=PACK)
-        for rows in (slice(0, 1), slice(1, PACK)):
+        for rows in (slice(0, 1), slice(1, 2), slice(2, PACK)):
             nc.vector.tensor_copy(dst[:, :VECTOR_GROUPS, :, rows], src[:, :VECTOR_GROUPS, :, rows])
             nc.scalar.copy(dst[:, VECTOR_GROUPS:, :, rows], src[:, VECTOR_GROUPS:, :, rows])
         w2_codes = keep.tile([P, H], U32, name="w2_codes", align_bytes=64)
@@ -126,6 +127,7 @@ def tile_picked_phlora_gelu_p_kernel(tc, x_words, x_scales, w1_words, w1_scales,
                     nc.scalar.activation(h[:].rearrange("p (n t) -> p n t", t=PACK)[:, part], pre[:].rearrange("p t n -> p n t")[:, part], GELU)
             hidden.append(h)
 
+        result = keep.tile([P, S], F32, name="result", align_bytes=64)
         for c in range(chunks):
             x_codes, x_bytes = x_operand(c)
             chunk_codes = keep.tile([P, CHUNK], U32, name=f"h_codes{c}", align_bytes=64)
@@ -137,9 +139,11 @@ def tile_picked_phlora_gelu_p_kernel(tc, x_words, x_scales, w1_words, w1_scales,
                                 rhs=x_codes, rhs_scale=x_bytes, start=True, stop=False)
             nc.tensor.matmul_mx(out=acc[:], lhsT=w3_codes.bitcast(FP4X4), lhsT_scale=w3_plane,
                                 rhs=chunk_codes[:].bitcast(FP8X4), rhs_scale=h_plane[:], start=False, stop=True)
-            result = keep.tile([P, CHUNK], F32, name=f"result{c}", align_bytes=64)
+            cols = slice(c * CHUNK, (c + 1) * CHUNK)
             if c == chunks - 1:
-                nc.vector.tensor_copy(result[:], acc[:])
+                nc.vector.tensor_copy(result[:, cols], acc[:])
             else:
-                nc.scalar.copy(result[:], acc[:])
-            nc.sync.dma_start(out[:, c * CHUNK:(c + 1) * CHUNK], result[:])
+                nc.scalar.copy(result[:, cols], acc[:])
+            if c > 0:
+                cols = slice(0 if c == 1 else cols.start, cols.stop)
+                nc.sync.dma_start(out[:, cols], result[:, cols])

@@ -52,8 +52,8 @@ def tile_picked_phlora_gelu_p_kernel(tc, x_words, x_scales, w1_words, w1_scales,
         offsets = keep.tile([P, S // LIST_ROWS], U16, name="offsets")
         nc.sync.dma_start(offsets[:], offs)
         nc.sync.dma_start(scale_table[0:P:BLOCK_ROWS, :].bitcast(I32), x_scales[0].bitcast(I32))
-        nc.sync.dma_start(w2_raw[:, 1:2], w2_rows[:, 1:2])
-        nc.sync.dma_start(w2_raw[:, 2:], w2_rows[:, 2:])
+        nc.sync.dma_start(w2_raw[:, 1:3], w2_rows[:, 1:3])
+        nc.sync.dma_start(w2_raw[:, 3:], w2_rows[:, 3:])
 
         word_table = keep.tile([P, T], I32, name="word_table", align_bytes=64)
         nc.sync.dma_start(word_table[:], x_words[0].rearrange("p n t -> p (n t)").bitcast(I32))
@@ -73,7 +73,7 @@ def tile_picked_phlora_gelu_p_kernel(tc, x_words, x_scales, w1_words, w1_scales,
         w2_bf = keep.tile([P, PACK * H], BF16, name="w2_bf", align_bytes=64)
         src = w2_raw[:].rearrange("p j (m t) -> p m t j", t=PACK)
         dst = w2_bf[:].rearrange("p (t m j) -> p m t j", t=PACK, j=PACK)
-        for rows in (slice(0, 1), slice(1, 2), slice(2, PACK)):
+        for rows in (slice(0, 1), slice(1, 3), slice(3, PACK)):
             nc.vector.tensor_copy(dst[:, :VECTOR_GROUPS, :, rows], src[:, :VECTOR_GROUPS, :, rows])
             nc.scalar.copy(dst[:, VECTOR_GROUPS:, :, rows], src[:, VECTOR_GROUPS:, :, rows])
         w2_codes = keep.tile([P, H], U32, name="w2_codes", align_bytes=64)

@@ -73,8 +73,9 @@ def tile_picked_phlora_gelu_p_kernel(tc, x_words, x_scales, w1_words, w1_scales,
         w2_bf = keep.tile([P, PACK * H], BF16, name="w2_bf", align_bytes=64)
         src = w2_raw[:].rearrange("p j (m t) -> p m t j", t=PACK)
         dst = w2_bf[:].rearrange("p (t m j) -> p m t j", t=PACK, j=PACK)
-        for rows in (slice(0, 1), slice(1, 3), slice(3, PACK)):
+        for rows in (slice(0, 3), slice(3, PACK)):
             nc.vector.tensor_copy(dst[:, :VECTOR_GROUPS, :, rows], src[:, :VECTOR_GROUPS, :, rows])
+        for rows in (slice(0, 1), slice(1, 3), slice(3, PACK)):
             nc.scalar.copy(dst[:, VECTOR_GROUPS:, :, rows], src[:, VECTOR_GROUPS:, :, rows])
         w2_codes = keep.tile([P, H], U32, name="w2_codes", align_bytes=64)
         w2_plane = keep.tile([P, H], U8, name="w2_plane", align_bytes=64)

@@ -21,7 +21,7 @@ LIST_ROWS = 16
 CHUNK = 128
 GATHER = 256
 VECTOR_GROUPS = 78
-WARM_PASSES = ((32, 128), (32, 128), (32, 128), (32, 128), (32, 512))
+WARM_PASSES = ((32, 128), (32, 128), (32, 128), (32, 128), (32, 512), (32, 128))
 FIRST_GROUPS = ((0, 1), (1, 2), (2, 4))
 ACC_TAGS = ("bank0_0", "bank0_1", "acc2", "acc3")
 FLOPS = 2 * S * (K * H + K * N + H * N)
@@ -73,10 +73,11 @@ def tile_picked_phlora_gelu_p_kernel(tc, x_words, x_scales, w1_words, w1_scales,
         w2_bf = keep.tile([P, PACK * H], BF16, name="w2_bf", align_bytes=64)
         src = w2_raw[:].rearrange("p j (m t) -> p m t j", t=PACK)
         dst = w2_bf[:].rearrange("p (t m j) -> p m t j", t=PACK, j=PACK)
-        for rows in (slice(0, 3), slice(3, PACK)):
-            nc.vector.tensor_copy(dst[:, :VECTOR_GROUPS, :, rows], src[:, :VECTOR_GROUPS, :, rows])
-        for rows in (slice(0, 1), slice(1, 3), slice(3, PACK)):
-            nc.scalar.copy(dst[:, VECTOR_GROUPS:, :, rows], src[:, VECTOR_GROUPS:, :, rows])
+        whole, first, rest = slice(0, PACK), slice(0, 1), slice(1, PACK)
+        for places, rows in ((whole, slice(0, 3)), (first, slice(3, PACK)), (rest, slice(3, PACK))):
+            nc.vector.tensor_copy(dst[:, :VECTOR_GROUPS, places, rows], src[:, :VECTOR_GROUPS, places, rows])
+        for places, rows in ((whole, slice(0, 1)), (whole, slice(1, 3)), (first, slice(3, PACK)), (rest, slice(3, PACK))):
+            nc.scalar.copy(dst[:, VECTOR_GROUPS:, places, rows], src[:, VECTOR_GROUPS:, places, rows])
         w2_codes = keep.tile([P, H], U32, name="w2_codes", align_bytes=64)
         w2_plane = keep.tile([P, H], U8, name="w2_plane", align_bytes=64)
         for cols in (slice(0, P), slice(P, 2 * P), slice(2 * P, H)):

@@ -129,16 +129,19 @@ def tile_picked_phlora_gelu_p_kernel(tc, x_words, x_scales, w1_words, w1_scales,
                     nc.scalar.activation(h[:].rearrange("p (n t) -> p n t", t=PACK)[:, part], pre[:].rearrange("p t n -> p n t")[:, part], GELU)
             hidden.append(h)
 
-        result = keep.tile([P, S], F32, name="result", align_bytes=64)
+        sums = []
         for c in range(chunks):
             x_codes, x_bytes = x_operand(c)
+            acc = psum.tile([P, CHUNK], F32, name=f"acc{c}", tag=ACC_TAGS[c])
+            nc.tensor.matmul_mx(out=acc[:], lhsT=w1_codes.bitcast(FP4X4), lhsT_scale=w1_plane,
+                                rhs=x_codes, rhs_scale=x_bytes, start=True, stop=False)
+            sums.append(acc)
+        result = keep.tile([P, S], F32, name="result", align_bytes=64)
+        for c, acc in enumerate(sums):
             chunk_codes = keep.tile([P, CHUNK], U32, name=f"h_codes{c}", align_bytes=64)
             h_plane = keep.tile([P, CHUNK], U8, name=f"h_plane{c}", align_bytes=64)
             for part in parts(c):
                 nc.vector.quantize_mx(out=chunk_codes[:, part].bitcast(FP8X4), scales=h_plane[:, part], in_=hidden[c][:, PACK * part.start:PACK * part.stop])
-            acc = psum.tile([P, CHUNK], F32, name=f"acc{c}", tag=ACC_TAGS[c])
-            nc.tensor.matmul_mx(out=acc[:], lhsT=w1_codes.bitcast(FP4X4), lhsT_scale=w1_plane,
-                                rhs=x_codes, rhs_scale=x_bytes, start=True, stop=False)
             nc.tensor.matmul_mx(out=acc[:], lhsT=w3_codes.bitcast(FP4X4), lhsT_scale=w3_plane,
                                 rhs=chunk_codes[:].bitcast(FP8X4), rhs_scale=h_plane[:], start=False, stop=True)
             cols = slice(c * CHUNK, (c + 1) * CHUNK)

@@ -21,7 +21,7 @@ LIST_ROWS = 16
 CHUNK = 128
 GATHER = 256
 VECTOR_GROUPS = 78
-WARM_PASSES = ((32, 128), (32, 128), (32, 128), (32, 128), (32, 512), (32, 128))
+WARM_PASSES = ((32, 128), (32, 128), (32, 128), (32, 128), (32, 128), (32, 512))
 FIRST_GROUPS = ((0, 1), (1, 2), (2, 4))
 ACC_TAGS = ("bank0_0", "bank0_1", "acc2", "acc3")
 FLOPS = 2 * S * (K * H + K * N + H * N)
@@ -80,7 +80,7 @@ def tile_picked_phlora_gelu_p_kernel(tc, x_words, x_scales, w1_words, w1_scales,
             nc.scalar.copy(dst[:, VECTOR_GROUPS:, places, rows], src[:, VECTOR_GROUPS:, places, rows])
         w2_codes = keep.tile([P, H], U32, name="w2_codes", align_bytes=64)
         w2_plane = keep.tile([P, H], U8, name="w2_plane", align_bytes=64)
-        for cols in (slice(0, P), slice(P, 2 * P), slice(2 * P, H)):
+        for cols in (slice(0, P), slice(P, H)):
             nc.vector.quantize_mx(out=w2_codes[:, cols].bitcast(FP8X4), scales=w2_plane[:, cols], in_=w2_bf[:, PACK * cols.start:PACK * cols.stop])
 
         warm_bank = psum.tile([P, S], F32, name="warm_bank", tag="last_bank")

@@ -20,7 +20,8 @@ QUADRANT = 32
 LIST_ROWS = 16
 CHUNK = 128
 GATHER = 256
-VECTOR_GROUPS = 78
+HALF = H // 2
+VECTOR_GROUPS = (0, 42)
 WARM_PASSES = ((32, 128), (32, 128), (32, 128), (32, 128), (32, 128), (32, 512))
 FIRST_GROUPS = ((0, 1), (1, 2), (2, 4))
 ACC_TAGS = ("bank0_0", "bank0_1", "acc2", "acc3")
@@ -46,14 +47,14 @@ def tile_picked_phlora_gelu_p_kernel(tc, x_words, x_scales, w1_words, w1_scales,
         warm_column = keep.tile([P, 1], F32, name="warm_column")
         nc.scalar.activation(warm_column[:], w1_plane[:, :4].bitcast(F32), GELU)
 
-        w2_raw = keep.tile([P, PACK, H], F32, name="w2_raw", align_bytes=64)
         w2_rows = w2.rearrange("(p j) c -> p j c", j=PACK)
-        nc.sync.dma_start(w2_raw[:, :1], w2_rows[:, :1])
+        raw = [keep.tile([P, PACK, HALF], F32, name=f"w2_raw{g}", align_bytes=64) for g in range(2)]
+        nc.sync.dma_start(raw[0][:, :2], w2_rows[:, :2, :HALF])
         offsets = keep.tile([P, S // LIST_ROWS], U16, name="offsets")
         nc.sync.dma_start(offsets[:], offs)
         nc.sync.dma_start(scale_table[0:P:BLOCK_ROWS, :].bitcast(I32), x_scales[0].bitcast(I32))
-        nc.sync.dma_start(w2_raw[:, 1:3], w2_rows[:, 1:3])
-        nc.sync.dma_start(w2_raw[:, 3:], w2_rows[:, 3:])
+        nc.sync.dma_start(raw[0][:, 2:], w2_rows[:, 2:, :HALF])
+        nc.sync.dma_start(raw[1][:], w2_rows[:, :, HALF:])
 
         word_table = keep.tile([P, T], I32, name="word_table", align_bytes=64)
         nc.sync.dma_start(word_table[:], x_words[0].rearrange("p n t -> p (n t)").bitcast(I32))
@@ -71,13 +72,13 @@ def tile_picked_phlora_gelu_p_kernel(tc, x_words, x_scales, w1_words, w1_scales,
                 nc.sync.dma_start(plane[i:P:QUADRANT, :].bitcast(I32), rows[0, i::rows_in_quadrant, :].bitcast(I32))
 
         w2_bf = keep.tile([P, PACK * H], BF16, name="w2_bf", align_bytes=64)
-        src = w2_raw[:].rearrange("p j (m t) -> p m t j", t=PACK)
-        dst = w2_bf[:].rearrange("p (t m j) -> p m t j", t=PACK, j=PACK)
-        whole, first, rest = slice(0, PACK), slice(0, 1), slice(1, PACK)
-        for places, rows in ((whole, slice(0, 3)), (first, slice(3, PACK)), (rest, slice(3, PACK))):
-            nc.vector.tensor_copy(dst[:, :VECTOR_GROUPS, places, rows], src[:, :VECTOR_GROUPS, places, rows])
-        for places, rows in ((whole, slice(0, 1)), (whole, slice(1, 3)), (first, slice(3, PACK)), (rest, slice(3, PACK))):
-            nc.scalar.copy(dst[:, VECTOR_GROUPS:, places, rows], src[:, VECTOR_GROUPS:, places, rows])
+        dealt = w2_bf[:].rearrange("p (t g m j) -> p g m t j", t=PACK, g=2, j=PACK)
+        for g in range(2):
+            src = raw[g][:].rearrange("p j (m t) -> p m t j", t=PACK)
+            share = VECTOR_GROUPS[g]
+            if share:
+                nc.vector.tensor_copy(dealt[:, g, :share], src[:, :share])
+            nc.scalar.copy(dealt[:, g, share:], src[:, share:])
         w2_codes = keep.tile([P, H], U32, name="w2_codes", align_bytes=64)
         w2_plane = keep.tile([P, H], U8, name="w2_plane", align_bytes=64)
         for cols in (slice(0, P), slice(P, H)):

@@ -20,9 +20,10 @@ QUADRANT = 32
 LIST_ROWS = 16
 CHUNK = 128
 GATHER = 256
-HALF = H // 2
-VECTOR_GROUPS = (0, 42)
-WARM_PASSES = ((32, 128), (32, 128), (32, 128), (32, 128), (32, 128), (32, 512))
+EARLY = 128
+LATE = H - EARLY
+VECTOR_GROUPS = (12, 62)
+WARM_PASSES = ((32, 128),) * 9
 FIRST_GROUPS = ((0, 1), (1, 2), (2, 4))
 ACC_TAGS = ("bank0_0", "bank0_1", "acc2", "acc3")
 FLOPS = 2 * S * (K * H + K * N + H * N)
@@ -40,6 +41,8 @@ def tile_picked_phlora_gelu_p_kernel(tc, x_words, x_scales, w1_words, w1_scales,
         x_plane = keep.tile([P, S], U8, name="x_plane", align_bytes=64)
         nc.vector.memset(x_plane[:].bitcast(I32), 0)
 
+        early_plane = keep.tile([P, EARLY], U8, name="early_plane", align_bytes=64)
+        nc.vector.memset(early_plane[:].bitcast(I32), 0)
         fp4 = keep.tile([P, 6 * N], U8, name="fp4", align_bytes=64)
         nc.vector.memset(fp4[:, :2 * N].bitcast(I32), 0)
         w1_plane, w3_plane, w1_codes, w3_codes = fp4[:, :N], fp4[:, N:2 * N], fp4[:, 2 * N:4 * N], fp4[:, 4 * N:]
@@ -47,14 +50,14 @@ def tile_picked_phlora_gelu_p_kernel(tc, x_words, x_scales, w1_words, w1_scales,
         warm_column = keep.tile([P, 1], F32, name="warm_column")
         nc.scalar.activation(warm_column[:], w1_plane[:, :4].bitcast(F32), GELU)
 
-        w2_rows = w2.rearrange("(p j) c -> p j c", j=PACK)
-        raw = [keep.tile([P, PACK, HALF], F32, name=f"w2_raw{g}", align_bytes=64) for g in range(2)]
-        nc.sync.dma_start(raw[0][:, :2], w2_rows[:, :2, :HALF])
+        w2_run = w2.rearrange("(p j) c -> p (j c)", j=PACK)
+        w2_raw = keep.tile([P, PACK * H], F32, name="w2_raw", align_bytes=64)
+        nc.sync.dma_start(w2_raw[:, 3 * H:], w2_run[:, 3 * H:])
         offsets = keep.tile([P, S // LIST_ROWS], U16, name="offsets")
         nc.sync.dma_start(offsets[:], offs)
         nc.sync.dma_start(scale_table[0:P:BLOCK_ROWS, :].bitcast(I32), x_scales[0].bitcast(I32))
-        nc.sync.dma_start(raw[0][:, 2:], w2_rows[:, 2:, :HALF])
-        nc.sync.dma_start(raw[1][:], w2_rows[:, :, HALF:])
+        nc.sync.dma_start(w2_raw[:, LATE:3 * H], w2_run[:, LATE:3 * H])
+        nc.sync.dma_start(w2_raw[:, :LATE], w2_run[:, :LATE])
 
         word_table = keep.tile([P, T], I32, name="word_table", align_bytes=64)
         nc.sync.dma_start(word_table[:], x_words[0].rearrange("p n t -> p (n t)").bitcast(I32))
@@ -71,23 +74,36 @@ def tile_picked_phlora_gelu_p_kernel(tc, x_words, x_scales, w1_words, w1_scales,
             for i in range(rows_in_quadrant):
                 nc.sync.dma_start(plane[i:P:QUADRANT, :].bitcast(I32), rows[0, i::rows_in_quadrant, :].bitcast(I32))
 
-        w2_bf = keep.tile([P, PACK * H], BF16, name="w2_bf", align_bytes=64)
-        dealt = w2_bf[:].rearrange("p (t g m j) -> p g m t j", t=PACK, g=2, j=PACK)
-        for g in range(2):
-            src = raw[g][:].rearrange("p j (m t) -> p m t j", t=PACK)
-            share = VECTOR_GROUPS[g]
-            if share:
-                nc.vector.tensor_copy(dealt[:, g, :share], src[:, :share])
-            nc.scalar.copy(dealt[:, g, share:], src[:, share:])
+        src = w2_raw[:].rearrange("p (j m t) -> p m t j", j=PACK, t=PACK)
+        late_groups = LATE // PACK
+        early_bf = keep.tile([P, PACK * EARLY], BF16, name="early_bf", align_bytes=64)
+        late_bf = keep.tile([P, PACK * LATE], BF16, name="late_bf", align_bytes=64)
+        early_codes = keep.tile([P, EARLY], U32, name="early_codes", align_bytes=64)
         w2_codes = keep.tile([P, H], U32, name="w2_codes", align_bytes=64)
         w2_plane = keep.tile([P, H], U8, name="w2_plane", align_bytes=64)
-        for cols in (slice(0, P), slice(P, H)):
-            nc.vector.quantize_mx(out=w2_codes[:, cols].bitcast(FP8X4), scales=w2_plane[:, cols], in_=w2_bf[:, PACK * cols.start:PACK * cols.stop])
+
+        def round_columns(rounded, columns, share):
+            dst = rounded[:].rearrange("p (t m j) -> p m t j", t=PACK, j=PACK)
+            nc.vector.tensor_copy(dst[:, :share], columns[:, :share])
+            nc.scalar.copy(dst[:, share:], columns[:, share:])
+
+        round_columns(early_bf, src[:, late_groups:], VECTOR_GROUPS[0])
+        nc.vector.quantize_mx(out=early_codes[:].bitcast(FP8X4), scales=early_plane[:], in_=early_bf[:])
+        round_columns(late_bf, src[:, :late_groups], VECTOR_GROUPS[1])
+        for dealt, staged in ((w2_codes, early_codes), (w2_plane, early_plane)):
+            places = dealt[:].bitcast(I32).rearrange("p (t m) -> p t m", t=PACK)
+            early = staged[:].bitcast(I32).rearrange("p (t m) -> p t m", t=PACK)
+            nc.vector.tensor_copy(places[:, :, places.shape[2] - early.shape[2]:], early)
+        for t in range(PACK):
+            for lo, hi in ((0, 64), (64, late_groups)):
+                cols = slice(t * P + lo, t * P + hi)
+                nc.vector.quantize_mx(out=w2_codes[:, cols].bitcast(FP8X4), scales=w2_plane[:, cols],
+                                      in_=late_bf[:, PACK * (t * late_groups + lo):PACK * (t * late_groups + hi)])
 
         warm_bank = psum.tile([P, S], F32, name="warm_bank", tag="last_bank")
         for rows, width in WARM_PASSES:
-            nc.tensor.matmul_mx(out=warm_bank[:rows, :width], lhsT=w2_codes[:, :rows].bitcast(FP8X4), lhsT_scale=w2_plane[:, :rows],
-                                rhs=w2_codes[:, :width].bitcast(FP8X4), rhs_scale=w2_plane[:, :width], start=True, stop=True)
+            nc.tensor.matmul_mx(out=warm_bank[:rows, :width], lhsT=early_codes[:, :rows].bitcast(FP8X4), lhsT_scale=early_plane[:, :rows],
+                                rhs=early_codes[:, :width].bitcast(FP8X4), rhs_scale=early_plane[:, :width], start=True, stop=True)
 
         picked_words = []
         for u in range(S // GATHER):

from contextlib import ExitStack

import concourse.mybir as mybir

F32 = mybir.dt.float32
BF16 = mybir.dt.bfloat16
I32 = mybir.dt.int32
U32 = mybir.dt.uint32
U16 = mybir.dt.uint16
U8 = mybir.dt.uint8
FP8X4 = mybir.dt.float8_e4m3fn_x4
FP4X4 = mybir.dt.float4_e2m1fn_x4
GELU = mybir.ActivationFunctionType.Gelu_apprx_tanh

P = 128
K, T, S, H, N = 512, 2048, 512, 512, 128
PACK = 4
BLOCK_ROWS = 8
QUADRANT = 32
LIST_ROWS = 16
CHUNK = 128
GATHER = 256
EARLY = 128
LATE = H - EARLY
VECTOR_GROUPS = (12, 62)
WARM_PASSES = ((32, 128),) * 9
FIRST_GROUPS = ((0, 1), (1, 2), (2, 4))
ACC_TAGS = ("bank0_0", "bank0_1", "acc2", "acc3")
FLOPS = 2 * S * (K * H + K * N + H * N)


def tile_picked_phlora_gelu_p_kernel(tc, x_words, x_scales, w1_words, w1_scales, w2, w3_words, w3_scales, offs, out):
    nc = tc.nc
    chunks = S // CHUNK
    with ExitStack() as ctx:
        keep = ctx.enter_context(tc.tile_pool(name="keep", bufs=1))
        psum = ctx.enter_context(tc.psum_pool(name="psum", bufs=1))

        scale_table = keep.tile([P, T], U8, name="scale_table", align_bytes=64)
        nc.vector.memset(scale_table[:].bitcast(I32), 0)
        x_plane = keep.tile([P, S], U8, name="x_plane", align_bytes=64)
        nc.vector.memset(x_plane[:].bitcast(I32), 0)

        early_plane = keep.tile([P, EARLY], U8, name="early_plane", align_bytes=64)
        nc.vector.memset(early_plane[:].bitcast(I32), 0)
        fp4 = keep.tile([P, 6 * N], U8, name="fp4", align_bytes=64)
        nc.vector.memset(fp4[:, :2 * N].bitcast(I32), 0)
        w1_plane, w3_plane, w1_codes, w3_codes = fp4[:, :N], fp4[:, N:2 * N], fp4[:, 2 * N:4 * N], fp4[:, 4 * N:]

        warm_column = keep.tile([P, 1], F32, name="warm_column")
        nc.scalar.activation(warm_column[:], w1_plane[:, :4].bitcast(F32), GELU)

        w2_run = w2.rearrange("(p j) c -> p (j c)", j=PACK)
        w2_raw = keep.tile([P, PACK * H], F32, name="w2_raw", align_bytes=64)
        nc.sync.dma_start(w2_raw[:, 3 * H:], w2_run[:, 3 * H:])
        offsets = keep.tile([P, S // LIST_ROWS], U16, name="offsets")
        nc.sync.dma_start(offsets[:], offs)
        nc.sync.dma_start(scale_table[0:P:BLOCK_ROWS, :].bitcast(I32), x_scales[0].bitcast(I32))
        nc.sync.dma_start(w2_raw[:, LATE:3 * H], w2_run[:, LATE:3 * H])
        nc.sync.dma_start(w2_raw[:, :LATE], w2_run[:, :LATE])

        word_table = keep.tile([P, T], I32, name="word_table", align_bytes=64)
        nc.sync.dma_start(word_table[:], x_words[0].rearrange("p n t -> p (n t)").bitcast(I32))

        picked_scales = keep.tile([P, S], U8, name="picked_scales", align_bytes=64)
        nc.vector.tensor_copy(picked_scales[:], scale_table[:].indirect(offsets[:]))
        rows_in_quadrant = QUADRANT // BLOCK_ROWS
        for i in range(rows_in_quadrant):
            nc.sync.dma_start(x_plane[i:P:QUADRANT, :].bitcast(I32), picked_scales[BLOCK_ROWS * i:P:QUADRANT, :].bitcast(I32))

        nc.sync.dma_start(w1_codes.bitcast(I32), w1_words[0].bitcast(I32))
        nc.sync.dma_start(w3_codes.bitcast(I32), w3_words[0].bitcast(I32))
        for plane, rows in ((w1_plane, w1_scales), (w3_plane, w3_scales)):
            for i in range(rows_in_quadrant):
                nc.sync.dma_start(plane[i:P:QUADRANT, :].bitcast(I32), rows[0, i::rows_in_quadrant, :].bitcast(I32))

        src = w2_raw[:].rearrange("p (j m t) -> p m t j", j=PACK, t=PACK)
        late_groups = LATE // PACK
        early_bf = keep.tile([P, PACK * EARLY], BF16, name="early_bf", align_bytes=64)
        late_bf = keep.tile([P, PACK * LATE], BF16, name="late_bf", align_bytes=64)
        early_codes = keep.tile([P, EARLY], U32, name="early_codes", align_bytes=64)
        w2_codes = keep.tile([P, H], U32, name="w2_codes", align_bytes=64)
        w2_plane = keep.tile([P, H], U8, name="w2_plane", align_bytes=64)

        def round_columns(rounded, columns, share):
            dst = rounded[:].rearrange("p (t m j) -> p m t j", t=PACK, j=PACK)
            nc.vector.tensor_copy(dst[:, :share], columns[:, :share])
            nc.scalar.copy(dst[:, share:], columns[:, share:])

        round_columns(early_bf, src[:, late_groups:], VECTOR_GROUPS[0])
        nc.vector.quantize_mx(out=early_codes[:].bitcast(FP8X4), scales=early_plane[:], in_=early_bf[:])
        round_columns(late_bf, src[:, :late_groups], VECTOR_GROUPS[1])
        for dealt, staged in ((w2_codes, early_codes), (w2_plane, early_plane)):
            places = dealt[:].bitcast(I32).rearrange("p (t m) -> p t m", t=PACK)
            early = staged[:].bitcast(I32).rearrange("p (t m) -> p t m", t=PACK)
            nc.vector.tensor_copy(places[:, :, places.shape[2] - early.shape[2]:], early)
        for t in range(PACK):
            for lo, hi in ((0, 64), (64, late_groups)):
                cols = slice(t * P + lo, t * P + hi)
                nc.vector.quantize_mx(out=w2_codes[:, cols].bitcast(FP8X4), scales=w2_plane[:, cols],
                                      in_=late_bf[:, PACK * (t * late_groups + lo):PACK * (t * late_groups + hi)])

        warm_bank = psum.tile([P, S], F32, name="warm_bank", tag="last_bank")
        for rows, width in WARM_PASSES:
            nc.tensor.matmul_mx(out=warm_bank[:rows, :width], lhsT=early_codes[:, :rows].bitcast(FP8X4), lhsT_scale=early_plane[:, :rows],
                                rhs=early_codes[:, :width].bitcast(FP8X4), rhs_scale=early_plane[:, :width], start=True, stop=True)

        picked_words = []
        for u in range(S // GATHER):
            words = keep.tile([P, GATHER], U32, name=f"picked_words{u}", align_bytes=64)
            entries = offsets[:, u * GATHER // LIST_ROWS:(u + 1) * GATHER // LIST_ROWS]
            nc.vector.tensor_copy(words[:], word_table[:].bitcast(U32).indirect(entries))
            picked_words.append(words)

        def x_operand(c):
            u, lo = divmod(c * CHUNK, GATHER)
            return picked_words[u][:, lo:lo + CHUNK].bitcast(FP8X4), x_plane[:, c * CHUNK:(c + 1) * CHUNK]

        def parts(c):
            if c == chunks - 1:
                return [slice(0, CHUNK // 2), slice(CHUNK // 2, CHUNK)]
            return [slice(0, CHUNK)]

        def first_pass(bank, c, t):
            x_codes, x_bytes = x_operand(c)
            cols = slice(t * P, (t + 1) * P)
            nc.tensor.matmul_mx(out=bank, lhsT=w2_codes[:, cols].bitcast(FP8X4), lhsT_scale=w2_plane[:, cols],
                                rhs=x_codes, rhs_scale=x_bytes, start=True, stop=True)

        hidden = []
        for c in range(chunks):
            h = keep.tile([P, CHUNK * PACK], BF16, name=f"h{c}", align_bytes=64)
            if c == 0:
                loose = keep.tile([P, PACK, CHUNK], BF16, name="loose", align_bytes=64)
                for u, (lo, hi) in enumerate(FIRST_GROUPS):
                    pre = psum.tile([P, hi - lo, CHUNK], F32, name=f"pre0_{u}", tag=f"bank0_{u}")
                    for t in range(lo, hi):
                        first_pass(pre[:, t - lo, :], c, t)
                    nc.scalar.activation(loose[:, lo:hi, :], pre[:], GELU)
                nc.vector.tensor_copy(h[:].rearrange("p (n u) -> p n u", u=PACK), loose[:].rearrange("p u n -> p n u"))
            else:
                pre = psum.tile([P, PACK, CHUNK], F32, name=f"pre{c}", tag="last_bank" if c == chunks - 1 else f"whole{c}")
                for t in range(PACK):
                    first_pass(pre[:, t, :], c, t)
                for part in parts(c):
                    nc.scalar.activation(h[:].rearrange("p (n t) -> p n t", t=PACK)[:, part], pre[:].rearrange("p t n -> p n t")[:, part], GELU)
            hidden.append(h)

        sums = []
        for c in range(chunks):
            x_codes, x_bytes = x_operand(c)
            acc = psum.tile([P, CHUNK], F32, name=f"acc{c}", tag=ACC_TAGS[c])
            nc.tensor.matmul_mx(out=acc[:], lhsT=w1_codes.bitcast(FP4X4), lhsT_scale=w1_plane,
                                rhs=x_codes, rhs_scale=x_bytes, start=True, stop=False)
            sums.append(acc)
        result = keep.tile([P, S], F32, name="result", align_bytes=64)
        for c, acc in enumerate(sums):
            chunk_codes = keep.tile([P, CHUNK], U32, name=f"h_codes{c}", align_bytes=64)
            h_plane = keep.tile([P, CHUNK], U8, name=f"h_plane{c}", align_bytes=64)
            for part in parts(c):
                nc.vector.quantize_mx(out=chunk_codes[:, part].bitcast(FP8X4), scales=h_plane[:, part], in_=hidden[c][:, PACK * part.start:PACK * part.stop])
            nc.tensor.matmul_mx(out=acc[:], lhsT=w3_codes.bitcast(FP4X4), lhsT_scale=w3_plane,
                                rhs=chunk_codes[:].bitcast(FP8X4), rhs_scale=h_plane[:], start=False, stop=True)
            cols = slice(c * CHUNK, (c + 1) * CHUNK)
            if c == chunks - 1:
                nc.vector.tensor_copy(result[:, cols], acc[:])
            else:
                nc.scalar.copy(result[:, cols], acc[:])
            if c > 0:
                cols = slice(0 if c == 1 else cols.start, cols.stop)
                nc.sync.dma_start(out[:, cols], result[:, cols])
